import numpy as np
import ml_dtypes


def mxq(x, axis, fmt="e4m3"):
    dtype, down = {"e4m3": (ml_dtypes.float8_e4m3fn, 7), "e5m2": (ml_dtypes.float8_e5m2, 14)}[fmt]
    v = np.moveaxis(np.asarray(x, np.float32).astype(ml_dtypes.bfloat16).astype(np.float64), axis, -1)
    blocks = v.reshape(v.shape[:-1] + (-1, 32))
    amax = np.abs(blocks).max(-1, keepdims=True)
    byte = np.maximum(np.where(amax > 0, np.frexp(amax)[1] - 1 + 127, 0) - down, 1)
    scale = np.exp2(byte - 127.0)
    codes = (blocks / scale).astype(np.float32).astype(dtype).astype(np.float64)
    return np.moveaxis((codes * scale).reshape(v.shape), -1, axis)


WIDE = False


def mx_kscale(k):
    if not WIDE:
        return np.ones(k)
    levels = np.array([10, -10, 5, -5, 0])
    if k % 512:
        return np.exp2(np.random.permutation(np.resize(levels, k // 32))).repeat(32)
    a = np.empty((k // 512, 16))
    for p in range(k // 512):
        a[p, :8] = np.random.permutation(np.resize(levels, 8))
        for g in range(8):
            far = levels[np.abs(levels - a[p, g]) >= 10]
            a[p, g + 8] = far[np.random.randint(len(far))]
    return np.exp2(a.ravel()).repeat(32)


def f64(x):
    return np.asarray(x).astype(np.float64)


def striped(idx):
    return np.tile(idx.reshape(-1, 16).T, (8, 1)).astype(np.uint16)


def unstriped(offs):
    return offs[:16].T.reshape(-1).astype(np.int64)


E2M1 = np.array([0.0, 0.5, 1.0, 1.5, 2.0, 3.0, 4.0, 6.0, -0.0, -0.5, -1.0, -1.5, -2.0, -3.0, -4.0, -6.0])


def pack_weight(w, fmt):
    k, n = w.shape
    w = f64(np.asarray(w, np.float32).astype(ml_dtypes.bfloat16)).reshape(k // 32, 32, n)
    amax = np.abs(w).max(1)
    if fmt == "e4m3":
        byte = np.frexp(amax)[1] - 1 + 127 - 7
    else:
        mant, ex = np.frexp(amax / 6.0)
        byte = np.where(mant > 0.5, ex, ex - 1) + 127
    byte = np.clip(np.where(amax > 0, byte, 1), 1, 254)
    scaled = (w * np.exp2(127.0 - byte)[:, None, :]).reshape(k, n).astype(np.float32)
    by_word = np.ascontiguousarray(scaled.reshape(k // 512, 128, 4, n).transpose(0, 1, 3, 2))
    if fmt == "e4m3":
        words = by_word.astype(ml_dtypes.float8_e4m3fn).view(np.uint8)
    else:
        c = by_word.astype(ml_dtypes.float4_e2m1fn).view(np.uint8) & 0xF
        words = (c[..., 0::2] | (c[..., 1::2] << 4)).reshape(k // 512, 128, 2 * n)
    return np.ascontiguousarray(words), np.ascontiguousarray(byte.astype(np.uint8).reshape(k // 512, 16, n))


def unpack_weight(words, scales, fmt):
    g, _, n = scales.shape
    words = np.ascontiguousarray(words).reshape(g, 128, n, -1)
    if fmt == "e4m3":
        vals = words.view(ml_dtypes.float8_e4m3fn).astype(np.float64)
    else:
        nib = np.empty((g, 128, n, 4), np.uint8)
        nib[..., 0::2] = words & 0xF
        nib[..., 1::2] = words >> 4
        vals = E2M1[nib]
    vals = vals * np.repeat(np.exp2(scales.astype(np.float64) - 127.0), 8, axis=1)[..., None]
    return vals.transpose(0, 1, 3, 2).reshape(g * 512, n)


def silu(v):
    return v / (1.0 + np.exp(-np.maximum(v, -700.0)))


K, T, E, C, N = 1536, 640, 15, 128, 128
TOP = 3


def by_expert(wq, xq):
    return np.concatenate([wq[e].T @ xq[:, e * C:(e + 1) * C] for e in range(E)], axis=1)


def setup_inputs():
    n = np.random.standard_normal
    s = mx_kscale(K)[:, None]
    deal = np.repeat(np.arange(E), C).reshape(TOP, T)[:, np.random.permutation(T)]
    deal = np.take_along_axis(deal, np.argsort(np.random.rand(TOP, T), axis=0), axis=0)
    for _ in range(8):
        s_, t_ = np.random.permutation(T).reshape(2, -1); r = np.random.randint(TOP, size=T // 2); x, y = deal[r, s_].copy(), deal[r, t_].copy()
        ok = ~((deal[:, s_] == y).any(0) | (deal[:, t_] == x).any(0)); deal[r[ok], s_[ok]] = y[ok]; deal[r[ok], t_[ok]] = x[ok]
    order = np.lexsort((np.random.rand(TOP * T), deal.reshape(-1)))
    slot_token = order % T; pos = np.empty(TOP * T, np.int64); pos[order] = np.arange(TOP * T); pos = pos.reshape(TOP, T)
    g = np.random.uniform(0.5, 1.5, (TOP, T)); g = g / g.sum(0)
    w = [pack_weight(m, "e2m1") for m in n((E, K, N)) / np.sqrt(K) / s[None]]
    return {
        "xT": (n((K, T)) * s).astype(np.float32),
        "w_words": np.stack([m[0] for m in w]),
        "w_scales": np.stack([m[1] for m in w]),
        "b": (0.3 * n((N, E))).astype(np.float32),
        "gate": np.stack([np.tile(r, (N, 1)) for r in g]).astype(np.float32),
        "offs": striped(slot_token),
        "pos1": striped(pos[0]),
        "pos2": striped(pos[1]),
        "pos3": striped(pos[2]),
    }


def reference(xT, w_words, w_scales, b, gate, offs, pos1, pos2, pos3):
    idx = unstriped(offs)
    w = np.stack([unpack_weight(w_words[e], w_scales[e], "e2m1") for e in range(E)])
    xq = mxq(f64(xT)[:, idx], 0, "e4m3")
    y = by_expert(w, xq)
    y = silu(y + np.repeat(f64(b), C, axis=1))
    return sum(f64(gate[r]) * y[:, unstriped(p)] for r, p in enumerate((pos1, pos2, pos3)))

@@ -1,0 +1,176 @@
+from contextlib import ExitStack
+
+import concourse.mybir as mybir
+
+K, T, E, C, N = 1536, 640, 15, 128, 128
+TOP = 3
+FLOPS = 2 * K * N * E * C
+
+P = 128
+PACK = 4
+A = 3
+S = E * C
+WIN = 2048
+
+F32 = mybir.dt.float32
+BF16 = mybir.dt.bfloat16
+U32 = mybir.dt.uint32
+I32 = mybir.dt.int32
+U16 = mybir.dt.uint16
+U8 = mybir.dt.uint8
+FP8X4 = mybir.dt.float8_e4m3fn_x4
+FP4X4 = mybir.dt.float4_e2m1fn_x4
+COPY = mybir.ActivationFunctionType.Copy
+SILU = mybir.ActivationFunctionType.Silu
+ADD = mybir.AluOpType.add
+MULT = mybir.AluOpType.mult
+
+
+def interleaved_views(dst, src):
+    return dst.rearrange("p (c i) j -> p c j i", i=4), src.rearrange("p j (c i) -> p c j i", i=4)
+
+
+def tile_moe_tk_lin_silu_kernel(
+    tc, xT, w_words, w_scales, b, gate, offs, pos1, pos2, pos3, out
+):
+    nc = tc.nc
+    with ExitStack() as ctx:
+        keep = ctx.enter_context(tc.tile_pool(name="keep", bufs=1))
+        psum = ctx.enter_context(tc.psum_pool(name="psum", bufs=8))
+
+        offs_sb = keep.tile([P, S // 16], U16, name="offs_sb")
+        pos_sb = [keep.tile([P, T // 16], U16, name=f"pos{r}_sb") for r in range(TOP)]
+        x_cuts = [[0, 384, 640], [0, 320, 640], [0, 320, 640]]
+        x_sb = [
+            [keep.tile([P, PACK, hi - lo], F32, name=f"x{a}_{lo}") for lo, hi in zip(x_cuts[a], x_cuts[a][1:])]
+            for a in range(A)
+        ]
+        xb = [keep.tile([P, T, PACK], BF16, name=f"xb{a}", align_bytes=64) for a in range(A)]
+        words = [keep.tile([P, WIN], U32, name=f"words{a}", align_bytes=64) for a in range(A)]
+        bytes3 = keep.tile([P, WIN], U8, name="bytes3", tag="late", align_bytes=64)
+        gwords = [keep.tile([P, S], U32, name=f"gwords{a}", align_bytes=64) for a in range(A)]
+        gbytes = [keep.tile([P, S], U8, name=f"gbytes{a}", align_bytes=64) for a in range(A)]
+        w_sb = keep.tile([P, E * A, 2 * N], U8, name="w_sb", align_bytes=64)
+        ws_sb = keep.tile([P, E * A, N], U8, name="ws_sb", align_bytes=64)
+        b_sb = keep.tile([P, E], F32, name="b_sb")
+        y_sb = keep.tile([P, S], F32, name="y_sb")
+        prod = [keep.tile([P, T], F32, name=f"prod{r}") for r in range(TOP)]
+        part = keep.tile([P, T], F32, name="part")
+        o_sb = keep.tile([P, T], F32, name="o_sb")
+        warm = keep.tile([P, 1], F32, name="warm")
+        warm_out = keep.tile([P, 1], F32, name="warm_out")
+
+        nc.vector.memset(warm[:], 0.0)
+        nc.scalar.activation(warm_out[:], warm[:], SILU)
+        nc.gpsimd.memset(bytes3[:, 0:T], 0)
+        nc.vector.memset(ws_sb[:].rearrange("p i n -> p (i n)").bitcast(I32), 0)
+        nc.gpsimd.memset(gbytes[1][:].bitcast(I32), 0)
+        nc.gpsimd.memset(gbytes[2][:].bitcast(I32), 0)
+
+        for a in range(A):
+            rows = xT[a * 512 : (a + 1) * 512, :].rearrange("(p j) t -> p j t", j=PACK)
+            for i, (lo, hi) in enumerate(zip(x_cuts[a], x_cuts[a][1:])):
+                nc.sync.dma_start(out=x_sb[a][i][:], in_=rows[:, :, lo:hi])
+            if a == 0:
+                nc.sync.dma_start(offs_sb[:], offs)
+            if a == 1:
+                nc.sync.dma_start(b_sb[:], b)
+        for q in range(4):
+            nc.sync.dma_start(
+                out=ws_sb[32 * q : 32 * q + 4].bitcast(I32),
+                in_=w_scales[:, :, 4 * q : 4 * q + 4, :].rearrange("e a q n -> q (e a) n").bitcast(I32),
+            )
+        for e0, e1 in ((0, 8), (8, E)):
+            nc.sync.dma_start(
+                out=w_sb[:, e0 * A : e1 * A, :].bitcast(I32),
+                in_=w_words[e0:e1].rearrange("e a p c -> p (e a) c").bitcast(I32),
+            )
+        for r, lst in enumerate((pos1, pos2, pos3)):
+            nc.sync.dma_start(pos_sb[r][:], lst)
+
+        def window(n):
+            return WIN if n >= 256 else T
+
+        def interleave(a, i, vector_columns):
+            lo, hi = x_cuts[a][i], x_cuts[a][i + 1]
+            mid = lo + vector_columns
+            if mid > lo:
+                dst, src = interleaved_views(xb[a][:, lo:mid, :], x_sb[a][i][:, :, 0 : mid - lo])
+                nc.vector.tensor_copy(dst, src)
+            for c0 in range(mid, hi, 320):
+                c1 = min(c0 + 320, hi)
+                dst, src = interleaved_views(xb[a][:, c0:c1, :], x_sb[a][i][:, :, c0 - lo : c1 - lo])
+                nc.scalar.activation(dst, src, COPY)
+
+        def quantize(a, lo, hi):
+            nc.vector.quantize_mx(
+                out=words[a][:, lo:hi].bitcast(FP8X4),
+                scales=bytes3[4 * a :, lo:hi],
+                in_=xb[a][:, lo:hi, :].rearrange("p t j -> p (t j)"),
+            )
+
+        def gather_words(a, lo, hi):
+            nc.vector.tensor_copy(gwords[a][:, lo:hi], words[a][:, 0 : window(hi - lo)].indirect(offs_sb[:, lo // 16 : hi // 16]))
+
+        def gather_bytes(lo, hi):
+            nc.vector.tensor_copy(gbytes[0][:, lo:hi], bytes3[:, 0 : window(hi - lo)].indirect(offs_sb[:, lo // 16 : hi // 16]))
+
+        def shift_bytes(lo, hi):
+            for a in (1, 2):
+                nc.scalar.dma_start(
+                    out=gbytes[a][0:112, lo:hi].bitcast(I32), in_=gbytes[0][4 * a : 4 * a + 112, lo:hi].bitcast(I32)
+                )
+
+        def expert(e):
+            cols = slice(e * C, (e + 1) * C)
+            acc = psum.tile([P, C], F32, name="acc")
+            for a in range(A):
+                i = e * A + a
+                nc.tensor.matmul_mx(
+                    out=acc[:],
+                    lhsT=w_sb[:, i, :].bitcast(FP4X4),
+                    lhsT_scale=ws_sb[:, i, :],
+                    rhs=gwords[a][:, cols].bitcast(FP8X4),
+                    rhs_scale=gbytes[a][:, cols],
+                    start=(a == 0),
+                    stop=(a == A - 1),
+                )
+            nc.scalar.activation(y_sb[:, cols], acc[:], SILU, bias=b_sb[:, e : e + 1])
+
+        interleave(0, 0, 256)
+        quantize(0, 0, 256)
+        interleave(0, 1, 176)
+        quantize(0, 256, 384)
+        quantize(0, 384, 640)
+        for i in range(2):
+            interleave(1, i, 0)
+        for i in range(2):
+            interleave(2, i, 0)
+        gather_words(0, 0, 1536)
+        gather_words(0, 1536, S)
+        quantize(1, 0, 512)
+        quantize(1, 512, 640)
+        gather_words(1, 0, 1152)
+        quantize(2, 0, 512)
+        quantize(2, 512, 640)
+        gather_bytes(0, 960)
+        shift_bytes(0, 960)
+        gather_bytes(960, 1920)
+        shift_bytes(960, 1920)
+        gate_sb = keep.tile([P, TOP, T], F32, name="gate_sb", tag="late", align_bytes=64)
+        nc.sync.dma_start(gate_sb[:], gate.rearrange("r p t -> p r t"))
+        for lo, hi in [(0, 384), (384, 768), (768, 1152), (1152, 1536), (1536, 1792), (1792, 1920)]:
+            if lo in (1152, 1536):
+                gather_words(1, lo, lo + 384)
+            gather_words(2, lo, hi)
+            for e in range(lo // C, hi // C):
+                expert(e)
+
+        for r in range(TOP):
+            nc.vector.tensor_tensor(prod[r][:], y_sb[:].indirect(pos_sb[r][:]), gate_sb[:, r, :], MULT)
+        halves = (slice(0, 320), slice(320, 640))
+        for ts in halves:
+            nc.vector.tensor_tensor(part[:, ts], prod[0][:, ts], prod[1][:, ts], ADD)
+        for ts in halves:
+            nc.vector.tensor_tensor(o_sb[:, ts], part[:, ts], prod[2][:, ts], ADD)
+            nc.sync.dma_start(out[:, ts], o_sb[:, ts])

@@ -11,6 +11,8 @@ PACK = 4
 A = 3
 S = E * C
 WIN = 2048
+HELD = 1536
+BANKS = 8
 
 F32 = mybir.dt.float32
 BF16 = mybir.dt.bfloat16
@@ -45,12 +47,16 @@ def tile_moe_tk_lin_silu_kernel(
             [keep.tile([P, PACK, hi - lo], F32, name=f"x{a}_{lo}") for lo, hi in zip(x_cuts[a], x_cuts[a][1:])]
             for a in range(A)
         ]
-        xb = [keep.tile([P, T, PACK], BF16, name=f"xb{a}", align_bytes=64) for a in range(A)]
+        xb = [keep.tile([P, T, PACK], BF16, name=f"xb{a}", tag=f"xb{a}", align_bytes=64) for a in range(A)]
         words = [keep.tile([P, WIN], U32, name=f"words{a}", align_bytes=64) for a in range(A)]
-        bytes3 = keep.tile([P, WIN], U8, name="bytes3", tag="late", align_bytes=64)
+        bytes3 = keep.tile([P, WIN], U8, name="bytes3", align_bytes=64)
         gwords = [keep.tile([P, S], U32, name=f"gwords{a}", align_bytes=64) for a in range(A)]
         gbytes = [keep.tile([P, S], U8, name=f"gbytes{a}", align_bytes=64) for a in range(A)]
-        w_sb = keep.tile([P, E * A, 2 * N], U8, name="w_sb", align_bytes=64)
+        w_cuts = [0, 3, 8, 12, E]
+        w_sb = [
+            keep.tile([P, (e1 - e0) * A, 2 * N], U8, name=f"w{e0}", tag=f"w{e0}", align_bytes=64)
+            for e0, e1 in zip(w_cuts, w_cuts[1:])
+        ]
         ws_sb = keep.tile([P, E * A, N], U8, name="ws_sb", align_bytes=64)
         b_sb = keep.tile([P, E], F32, name="b_sb")
         y_sb = keep.tile([P, S], F32, name="y_sb")
@@ -74,19 +80,19 @@ def tile_moe_tk_lin_silu_kernel(
             if a == 0:
                 nc.sync.dma_start(offs_sb[:], offs)
             if a == 1:
+                nc.sync.dma_start(
+                    out=ws_sb[0:P:8].bitcast(I32), in_=w_scales.rearrange("e a q n -> q (e a) n").bitcast(I32)
+                )
+                for r, lst in enumerate((pos1, pos2, pos3)):
+                    nc.sync.dma_start(pos_sb[r][:], lst)
                 nc.sync.dma_start(b_sb[:], b)
-        for q in range(4):
+        for i, (e0, e1) in enumerate(zip(w_cuts, w_cuts[1:])):
             nc.sync.dma_start(
-                out=ws_sb[32 * q : 32 * q + 4].bitcast(I32),
-                in_=w_scales[:, :, 4 * q : 4 * q + 4, :].rearrange("e a q n -> q (e a) n").bitcast(I32),
-            )
-        for e0, e1 in ((0, 8), (8, E)):
-            nc.sync.dma_start(
-                out=w_sb[:, e0 * A : e1 * A, :].bitcast(I32),
+                out=w_sb[i][:].bitcast(I32),
                 in_=w_words[e0:e1].rearrange("e a p c -> p (e a) c").bitcast(I32),
             )
-        for r, lst in enumerate((pos1, pos2, pos3)):
-            nc.sync.dma_start(pos_sb[r][:], lst)
+
+        held = []
 
         def window(n):
             return WIN if n >= 256 else T
@@ -109,8 +115,13 @@ def tile_moe_tk_lin_silu_kernel(
                 in_=xb[a][:, lo:hi, :].rearrange("p t j -> p (t j)"),
             )
 
+        def slot_words(a, lo, hi):
+            if a == 1 and lo >= HELD:
+                return held[0][:, lo - HELD : hi - HELD]
+            return gwords[a][:, lo:hi]
+
         def gather_words(a, lo, hi):
-            nc.vector.tensor_copy(gwords[a][:, lo:hi], words[a][:, 0 : window(hi - lo)].indirect(offs_sb[:, lo // 16 : hi // 16]))
+            nc.vector.tensor_copy(slot_words(a, lo, hi), words[a][:, 0 : window(hi - lo)].indirect(offs_sb[:, lo // 16 : hi // 16]))
 
         def gather_bytes(lo, hi):
             nc.vector.tensor_copy(gbytes[0][:, lo:hi], bytes3[:, 0 : window(hi - lo)].indirect(offs_sb[:, lo // 16 : hi // 16]))
@@ -121,21 +132,27 @@ def tile_moe_tk_lin_silu_kernel(
                     out=gbytes[a][0:112, lo:hi].bitcast(I32), in_=gbytes[0][4 * a : 4 * a + 112, lo:hi].bitcast(I32)
                 )
 
-        def expert(e):
+        acc = {}
+
+        def multiply(e, a):
             cols = slice(e * C, (e + 1) * C)
-            acc = psum.tile([P, C], F32, name="acc")
-            for a in range(A):
-                i = e * A + a
-                nc.tensor.matmul_mx(
-                    out=acc[:],
-                    lhsT=w_sb[:, i, :].bitcast(FP4X4),
-                    lhsT_scale=ws_sb[:, i, :],
-                    rhs=gwords[a][:, cols].bitcast(FP8X4),
-                    rhs_scale=gbytes[a][:, cols],
-                    start=(a == 0),
-                    stop=(a == A - 1),
-                )
-            nc.scalar.activation(y_sb[:, cols], acc[:], SILU, bias=b_sb[:, e : e + 1])
+            if a == 0:
+                acc[e] = psum.tile([P, C], F32, name="acc")
+            piece = max(j for j, e0 in enumerate(w_cuts) if e0 <= e)
+            i = e * A + a
+            nc.tensor.matmul_mx(
+                out=acc[e][:],
+                lhsT=w_sb[piece][:, i - w_cuts[piece] * A, :].bitcast(FP4X4),
+                lhsT_scale=ws_sb[:, i, :],
+                rhs=slot_words(a, e * C, (e + 1) * C).bitcast(FP8X4),
+                rhs_scale=gbytes[a][:, cols],
+                start=(a == 0),
+                stop=(a == A - 1),
+            )
+            if a == A - 1:
+                nc.scalar.activation(y_sb[:, cols], acc[e][:], SILU, bias=b_sb[:, e : e + 1])
+                if e + BANKS < E:
+                    multiply(e + BANKS, 0)
 
         interleave(0, 0, 256)
         quantize(0, 0, 256)
@@ -144,28 +161,41 @@ def tile_moe_tk_lin_silu_kernel(
         quantize(0, 384, 640)
         for i in range(2):
             interleave(1, i, 0)
+        ws_rows = ws_sb[:].rearrange("p i n -> p (i n)").bitcast(I32)
+        for r in range(1, 4):
+            nc.scalar.dma_start(out=ws_rows[r:P:32], in_=ws_rows[8 * r : P : 32])
         for i in range(2):
             interleave(2, i, 0)
         gather_words(0, 0, 1536)
         gather_words(0, 1536, S)
         quantize(1, 0, 512)
         quantize(1, 512, 640)
-        gather_words(1, 0, 1152)
+        gather_words(1, 0, HELD)
         quantize(2, 0, 512)
         quantize(2, 512, 640)
+        held.append(keep.tile([P, S - HELD], U32, name="held", tag="xb2", align_bytes=64))
         gather_bytes(0, 960)
         shift_bytes(0, 960)
         gather_bytes(960, 1920)
         shift_bytes(960, 1920)
-        gate_sb = keep.tile([P, TOP, T], F32, name="gate_sb", tag="late", align_bytes=64)
-        nc.sync.dma_start(gate_sb[:], gate.rearrange("r p t -> p r t"))
-        for lo, hi in [(0, 384), (384, 768), (768, 1152), (1152, 1536), (1536, 1792), (1792, 1920)]:
-            if lo in (1152, 1536):
-                gather_words(1, lo, lo + 384)
+        for e in range(BANKS):
+            multiply(e, 0)
+        for lo, hi in [(0, 384), (384, 768), (768, 1152), (1152, HELD)]:
             gather_words(2, lo, hi)
             for e in range(lo // C, hi // C):
-                expert(e)
+                multiply(e, 1)
+                multiply(e, 2)
+        gather_words(1, HELD, S)
+        for e in range(HELD // C, E):
+            multiply(e, 1)
+        for lo, hi in [(HELD, 1792), (1792, S)]:
+            gather_words(2, lo, hi)
+            for e in range(lo // C, hi // C):
+                multiply(e, 2)
 
+        gate_sb = keep.tile([P, TOP, T], F32, name="gate_sb", tag="w0", align_bytes=64)
+        for r in range(TOP):
+            nc.sync.dma_start(gate_sb[:, r, :], gate[r])
         for r in range(TOP):
             nc.vector.tensor_tensor(prod[r][:], y_sb[:].indirect(pos_sb[r][:]), gate_sb[:, r, :], MULT)
         halves = (slice(0, 320), slice(320, 640))

@@ -42,7 +42,7 @@ def tile_moe_tk_lin_silu_kernel(
 
         offs_sb = keep.tile([P, S // 16], U16, name="offs_sb")
         pos_sb = [keep.tile([P, T // 16], U16, name=f"pos{r}_sb") for r in range(TOP)]
-        x_cuts = [[0, 384, 640], [0, 320, 640], [0, 320, 640]]
+        x_cuts = [[0, 384, 640], [0, 640], [0, 640]]
         x_sb = [
             [keep.tile([P, PACK, hi - lo], F32, name=f"x{a}_{lo}") for lo, hi in zip(x_cuts[a], x_cuts[a][1:])]
             for a in range(A)
@@ -52,7 +52,7 @@ def tile_moe_tk_lin_silu_kernel(
         bytes3 = keep.tile([P, WIN], U8, name="bytes3", align_bytes=64)
         gwords = [keep.tile([P, S], U32, name=f"gwords{a}", align_bytes=64) for a in range(A)]
         gbytes = [keep.tile([P, S], U8, name=f"gbytes{a}", align_bytes=64) for a in range(A)]
-        w_cuts = [0, 3, 8, 12, E]
+        w_cuts = [0, 3, 8, 13, E]
         w_sb = [
             keep.tile([P, (e1 - e0) * A, 2 * N], U8, name=f"w{e0}", tag=f"w{e0}", align_bytes=64)
             for e0, e1 in zip(w_cuts, w_cuts[1:])
@@ -83,14 +83,14 @@ def tile_moe_tk_lin_silu_kernel(
                 nc.sync.dma_start(
                     out=ws_sb[0:P:8].bitcast(I32), in_=w_scales.rearrange("e a q n -> q (e a) n").bitcast(I32)
                 )
-                for r, lst in enumerate((pos1, pos2, pos3)):
-                    nc.sync.dma_start(pos_sb[r][:], lst)
                 nc.sync.dma_start(b_sb[:], b)
         for i, (e0, e1) in enumerate(zip(w_cuts, w_cuts[1:])):
             nc.sync.dma_start(
                 out=w_sb[i][:].bitcast(I32),
                 in_=w_words[e0:e1].rearrange("e a p c -> p (e a) c").bitcast(I32),
             )
+        for r, lst in enumerate((pos1, pos2, pos3)):
+            nc.sync.dma_start(pos_sb[r][:], lst)
 
         held = []
 
@@ -159,13 +159,11 @@ def tile_moe_tk_lin_silu_kernel(
         interleave(0, 1, 176)
         quantize(0, 256, 384)
         quantize(0, 384, 640)
-        for i in range(2):
-            interleave(1, i, 0)
+        interleave(1, 0, 0)
         ws_rows = ws_sb[:].rearrange("p i n -> p (i n)").bitcast(I32)
         for r in range(1, 4):
             nc.scalar.dma_start(out=ws_rows[r:P:32], in_=ws_rows[8 * r : P : 32])
-        for i in range(2):
-            interleave(2, i, 0)
+        interleave(2, 0, 0)
         gather_words(0, 0, 1536)
         gather_words(0, 1536, S)
         quantize(1, 0, 512)

@@ -11,7 +11,7 @@ PACK = 4
 A = 3
 S = E * C
 WIN = 2048
-HELD = 1536
+HELD = 1280
 BANKS = 8
 
 F32 = mybir.dt.float32
@@ -42,7 +42,7 @@ def tile_moe_tk_lin_silu_kernel(
 
         offs_sb = keep.tile([P, S // 16], U16, name="offs_sb")
         pos_sb = [keep.tile([P, T // 16], U16, name=f"pos{r}_sb") for r in range(TOP)]
-        x_cuts = [[0, 384, 640], [0, 640], [0, 640]]
+        x_cuts = [[0, 384, 640], [0, 320, 640], [0, 320, 640]]
         x_sb = [
             [keep.tile([P, PACK, hi - lo], F32, name=f"x{a}_{lo}") for lo, hi in zip(x_cuts[a], x_cuts[a][1:])]
             for a in range(A)
@@ -63,11 +63,7 @@ def tile_moe_tk_lin_silu_kernel(
         prod = [keep.tile([P, T], F32, name=f"prod{r}") for r in range(TOP)]
         part = keep.tile([P, T], F32, name="part")
         o_sb = keep.tile([P, T], F32, name="o_sb")
-        warm = keep.tile([P, 1], F32, name="warm")
-        warm_out = keep.tile([P, 1], F32, name="warm_out")
 
-        nc.vector.memset(warm[:], 0.0)
-        nc.scalar.activation(warm_out[:], warm[:], SILU)
         nc.gpsimd.memset(bytes3[:, 0:T], 0)
         nc.vector.memset(ws_sb[:].rearrange("p i n -> p (i n)").bitcast(I32), 0)
         nc.gpsimd.memset(gbytes[1][:].bitcast(I32), 0)
@@ -159,11 +155,13 @@ def tile_moe_tk_lin_silu_kernel(
         interleave(0, 1, 176)
         quantize(0, 256, 384)
         quantize(0, 384, 640)
-        interleave(1, 0, 0)
+        for i in range(2):
+            interleave(1, i, 0)
         ws_rows = ws_sb[:].rearrange("p i n -> p (i n)").bitcast(I32)
         for r in range(1, 4):
             nc.scalar.dma_start(out=ws_rows[r:P:32], in_=ws_rows[8 * r : P : 32])
-        interleave(2, 0, 0)
+        for i in range(2):
+            interleave(2, i, 0)
         gather_words(0, 0, 1536)
         gather_words(0, 1536, S)
         quantize(1, 0, 512)
@@ -178,15 +176,16 @@ def tile_moe_tk_lin_silu_kernel(
         shift_bytes(960, 1920)
         for e in range(BANKS):
             multiply(e, 0)
-        for lo, hi in [(0, 384), (384, 768), (768, 1152), (1152, HELD)]:
+        for e in range(7):
+            multiply(e, 1)
+        for lo, hi in [(0, 384), (384, 896)]:
             gather_words(2, lo, hi)
             for e in range(lo // C, hi // C):
-                multiply(e, 1)
                 multiply(e, 2)
         gather_words(1, HELD, S)
-        for e in range(HELD // C, E):
+        for e in range(7, E):
             multiply(e, 1)
-        for lo, hi in [(HELD, 1792), (1792, S)]:
+        for lo, hi in [(896, 1408), (1408, 1792), (1792, S)]:
             gather_words(2, lo, hi)
             for e in range(lo // C, hi // C):
                 multiply(e, 2)

@@ -11,7 +11,7 @@ PACK = 4
 A = 3
 S = E * C
 WIN = 2048
-HELD = 1280
+HELD = 1408
 BANKS = 8
 
 F32 = mybir.dt.float32
@@ -42,7 +42,7 @@ def tile_moe_tk_lin_silu_kernel(
 
         offs_sb = keep.tile([P, S // 16], U16, name="offs_sb")
         pos_sb = [keep.tile([P, T // 16], U16, name=f"pos{r}_sb") for r in range(TOP)]
-        x_cuts = [[0, 384, 640], [0, 320, 640], [0, 320, 640]]
+        x_cuts = [[0, 384, 640], [0, 320, 640], [0, 384, 640]]
         x_sb = [
             [keep.tile([P, PACK, hi - lo], F32, name=f"x{a}_{lo}") for lo, hi in zip(x_cuts[a], x_cuts[a][1:])]
             for a in range(A)
@@ -73,13 +73,13 @@ def tile_moe_tk_lin_silu_kernel(
             rows = xT[a * 512 : (a + 1) * 512, :].rearrange("(p j) t -> p j t", j=PACK)
             for i, (lo, hi) in enumerate(zip(x_cuts[a], x_cuts[a][1:])):
                 nc.sync.dma_start(out=x_sb[a][i][:], in_=rows[:, :, lo:hi])
+                if (a, i) == (2, 0):
+                    nc.sync.dma_start(
+                        out=ws_sb[0:P:8].bitcast(I32), in_=w_scales.rearrange("e a q n -> q (e a) n").bitcast(I32)
+                    )
             if a == 0:
                 nc.sync.dma_start(offs_sb[:], offs)
-            if a == 1:
-                nc.sync.dma_start(
-                    out=ws_sb[0:P:8].bitcast(I32), in_=w_scales.rearrange("e a q n -> q (e a) n").bitcast(I32)
-                )
-                nc.sync.dma_start(b_sb[:], b)
+        nc.sync.dma_start(b_sb[:], b)
         for i, (e0, e1) in enumerate(zip(w_cuts, w_cuts[1:])):
             nc.sync.dma_start(
                 out=w_sb[i][:].bitcast(I32),
@@ -99,8 +99,8 @@ def tile_moe_tk_lin_silu_kernel(
             if mid > lo:
                 dst, src = interleaved_views(xb[a][:, lo:mid, :], x_sb[a][i][:, :, 0 : mid - lo])
                 nc.vector.tensor_copy(dst, src)
-            for c0 in range(mid, hi, 320):
-                c1 = min(c0 + 320, hi)
+            if hi > mid:
+                c0, c1 = mid, hi
                 dst, src = interleaved_views(xb[a][:, c0:c1, :], x_sb[a][i][:, :, c0 - lo : c1 - lo])
                 nc.scalar.activation(dst, src, COPY)
 
@@ -122,9 +122,9 @@ def tile_moe_tk_lin_silu_kernel(
         def gather_bytes(lo, hi):
             nc.vector.tensor_copy(gbytes[0][:, lo:hi], bytes3[:, 0 : window(hi - lo)].indirect(offs_sb[:, lo // 16 : hi // 16]))
 
-        def shift_bytes(lo, hi):
+        def shift_bytes(lo, hi, queue):
             for a in (1, 2):
-                nc.scalar.dma_start(
+                queue.dma_start(
                     out=gbytes[a][0:112, lo:hi].bitcast(I32), in_=gbytes[0][4 * a : 4 * a + 112, lo:hi].bitcast(I32)
                 )
 
@@ -157,11 +157,11 @@ def tile_moe_tk_lin_silu_kernel(
         quantize(0, 384, 640)
         for i in range(2):
             interleave(1, i, 0)
+        for i in range(2):
+            interleave(2, i, 0)
         ws_rows = ws_sb[:].rearrange("p i n -> p (i n)").bitcast(I32)
         for r in range(1, 4):
             nc.scalar.dma_start(out=ws_rows[r:P:32], in_=ws_rows[8 * r : P : 32])
-        for i in range(2):
-            interleave(2, i, 0)
         gather_words(0, 0, 1536)
         gather_words(0, 1536, S)
         quantize(1, 0, 512)
@@ -171,9 +171,9 @@ def tile_moe_tk_lin_silu_kernel(
         quantize(2, 512, 640)
         held.append(keep.tile([P, S - HELD], U32, name="held", tag="xb2", align_bytes=64))
         gather_bytes(0, 960)
-        shift_bytes(0, 960)
+        shift_bytes(0, 960, nc.scalar)
         gather_bytes(960, 1920)
-        shift_bytes(960, 1920)
+        shift_bytes(960, 1920, nc.sync)
         for e in range(BANKS):
             multiply(e, 0)
         for e in range(7):
@@ -182,10 +182,14 @@ def tile_moe_tk_lin_silu_kernel(
             gather_words(2, lo, hi)
             for e in range(lo // C, hi // C):
                 multiply(e, 2)
+        gather_words(2, 896, HELD)
+        for a in (1, 2):
+            for e in range(7, HELD // C):
+                multiply(e, a)
         gather_words(1, HELD, S)
-        for e in range(7, E):
+        for e in range(HELD // C, E):
             multiply(e, 1)
-        for lo, hi in [(896, 1408), (1408, 1792), (1792, S)]:
+        for lo, hi in [(HELD, 1664), (1664, 1792), (1792, S)]:
             gather_words(2, lo, hi)
             for e in range(lo // C, hi // C):
                 multiply(e, 2)

@@ -8,11 +8,18 @@ FLOPS = 2 * K * N * E * C
 
 P = 128
 PACK = 4
-A = 3
+PASSES = K // (P * PACK)
 S = E * C
-WIN = 2048
-HELD = 1408
 BANKS = 8
+PER_COLUMN = 16
+PLANE_STEP = 4
+PLANE_ROWS = 100
+
+X_CUTS = [[0, 384, T], [0, 320, T], [0, 384, T]]
+VECTOR_TOKENS = (256, 176)
+W_CUTS = [0, 3, BANKS, 13, E]
+HELD = 11 * C
+FIRST_HALF = (S // 2) // C
 
 F32 = mybir.dt.float32
 BF16 = mybir.dt.bfloat16
@@ -32,100 +39,114 @@ def interleaved_views(dst, src):
     return dst.rearrange("p (c i) j -> p c j i", i=4), src.rearrange("p j (c i) -> p c j i", i=4)
 
 
+def window_columns(offsets):
+    if offsets > 1536:
+        return 4096
+    return 2048 if offsets >= 256 else T
+
+
 def tile_moe_tk_lin_silu_kernel(
     tc, xT, w_words, w_scales, b, gate, offs, pos1, pos2, pos3, out
 ):
     nc = tc.nc
     with ExitStack() as ctx:
         keep = ctx.enter_context(tc.tile_pool(name="keep", bufs=1))
-        psum = ctx.enter_context(tc.psum_pool(name="psum", bufs=8))
+        psum = ctx.enter_context(tc.psum_pool(name="psum", bufs=BANKS))
 
-        offs_sb = keep.tile([P, S // 16], U16, name="offs_sb")
-        pos_sb = [keep.tile([P, T // 16], U16, name=f"pos{r}_sb") for r in range(TOP)]
-        x_cuts = [[0, 384, 640], [0, 320, 640], [0, 384, 640]]
+        offs_sb = keep.tile([P, S // PER_COLUMN], U16, name="offs_sb")
+        pos_sb = [keep.tile([P, T // PER_COLUMN], U16, name=f"pos{r}_sb") for r in range(TOP)]
         x_sb = [
-            [keep.tile([P, PACK, hi - lo], F32, name=f"x{a}_{lo}") for lo, hi in zip(x_cuts[a], x_cuts[a][1:])]
-            for a in range(A)
+            [
+                keep.tile([P, PACK, hi - lo], F32, name=f"x{a}_{i}", tag=f"x{a}_{i}", align_bytes=64)
+                for i, (lo, hi) in enumerate(zip(X_CUTS[a], X_CUTS[a][1:]))
+            ]
+            for a in range(PASSES)
         ]
-        xb = [keep.tile([P, T, PACK], BF16, name=f"xb{a}", tag=f"xb{a}", align_bytes=64) for a in range(A)]
-        words = [keep.tile([P, WIN], U32, name=f"words{a}", align_bytes=64) for a in range(A)]
-        bytes3 = keep.tile([P, WIN], U8, name="bytes3", align_bytes=64)
-        gwords = [keep.tile([P, S], U32, name=f"gwords{a}", align_bytes=64) for a in range(A)]
-        gbytes = [keep.tile([P, S], U8, name=f"gbytes{a}", align_bytes=64) for a in range(A)]
-        w_cuts = [0, 3, 8, 13, E]
+        rounded = [
+            keep.tile([P, T, PACK], BF16, name=f"rounded{a}", tag=f"rounded{a}", align_bytes=64) for a in range(PASSES)
+        ]
+        token_words = [
+            keep.tile([P, window_columns(S - C if a == 0 else HELD)], U32, name=f"token_words{a}", align_bytes=64)
+            for a in range(PASSES)
+        ]
+        token_scales = keep.tile([P, window_columns(S // 2)], U8, name="token_scales", align_bytes=64)
+        slot_words = [keep.tile([P, S], U32, name=f"slot_words{a}", align_bytes=64) for a in range(PASSES)]
+        slot_scales = [keep.tile([P, S], U8, name=f"slot_scales{a}", align_bytes=64) for a in range(PASSES)]
         w_sb = [
-            keep.tile([P, (e1 - e0) * A, 2 * N], U8, name=f"w{e0}", tag=f"w{e0}", align_bytes=64)
-            for e0, e1 in zip(w_cuts, w_cuts[1:])
+            keep.tile([P, (e1 - e0) * PASSES, 2 * N], U8, name=f"w{e0}", tag=f"w{e0}", align_bytes=64)
+            for e0, e1 in zip(W_CUTS, W_CUTS[1:])
         ]
-        ws_sb = keep.tile([P, E * A, N], U8, name="ws_sb", align_bytes=64)
+        w_planes = keep.tile([P, E * PASSES, N], U8, name="w_planes", align_bytes=64)
         b_sb = keep.tile([P, E], F32, name="b_sb")
         y_sb = keep.tile([P, S], F32, name="y_sb")
         prod = [keep.tile([P, T], F32, name=f"prod{r}") for r in range(TOP)]
         part = keep.tile([P, T], F32, name="part")
-        o_sb = keep.tile([P, T], F32, name="o_sb")
+        out_sb = keep.tile([P, T], F32, name="out_sb")
 
-        nc.gpsimd.memset(bytes3[:, 0:T], 0)
-        nc.vector.memset(ws_sb[:].rearrange("p i n -> p (i n)").bitcast(I32), 0)
-        nc.gpsimd.memset(gbytes[1][:].bitcast(I32), 0)
-        nc.gpsimd.memset(gbytes[2][:].bitcast(I32), 0)
+        w_plane_rows = w_planes[:].rearrange("p i n -> p (i n)").bitcast(I32)
+        nc.vector.memset(w_plane_rows, 0)
+        nc.vector.memset(token_scales[:, 0:T].bitcast(I32), 0)
+        for a in range(1, PASSES):
+            nc.vector.memset(slot_scales[a][:].bitcast(I32), 0)
 
-        for a in range(A):
-            rows = xT[a * 512 : (a + 1) * 512, :].rearrange("(p j) t -> p j t", j=PACK)
-            for i, (lo, hi) in enumerate(zip(x_cuts[a], x_cuts[a][1:])):
+        for a in range(PASSES):
+            rows = xT[a * P * PACK : (a + 1) * P * PACK, :].rearrange("(p j) t -> p j t", j=PACK)
+            for i, (lo, hi) in enumerate(zip(X_CUTS[a], X_CUTS[a][1:])):
                 nc.sync.dma_start(out=x_sb[a][i][:], in_=rows[:, :, lo:hi])
-                if (a, i) == (2, 0):
+                if (a, i) == (PASSES - 1, 0):
                     nc.sync.dma_start(
-                        out=ws_sb[0:P:8].bitcast(I32), in_=w_scales.rearrange("e a q n -> q (e a) n").bitcast(I32)
+                        out=w_planes[0:P:8].bitcast(I32),
+                        in_=w_scales.rearrange("e a q n -> q (e a) n").bitcast(I32),
                     )
             if a == 0:
                 nc.sync.dma_start(offs_sb[:], offs)
         nc.sync.dma_start(b_sb[:], b)
-        for i, (e0, e1) in enumerate(zip(w_cuts, w_cuts[1:])):
+        for i, (e0, e1) in enumerate(zip(W_CUTS, W_CUTS[1:])):
             nc.sync.dma_start(
                 out=w_sb[i][:].bitcast(I32),
                 in_=w_words[e0:e1].rearrange("e a p c -> p (e a) c").bitcast(I32),
             )
-        for r, lst in enumerate((pos1, pos2, pos3)):
-            nc.sync.dma_start(pos_sb[r][:], lst)
+        for r, positions in enumerate((pos1, pos2, pos3)):
+            nc.sync.dma_start(pos_sb[r][:], positions)
 
-        held = []
+        apart = {}
 
-        def window(n):
-            return WIN if n >= 256 else T
+        def gathered(a, lo, hi):
+            for (pass_apart, first), tile in apart.items():
+                if pass_apart == a and first <= lo < first + tile.shape[1]:
+                    return tile[:, lo - first : hi - first]
+            return slot_words[a][:, lo:hi]
 
-        def interleave(a, i, vector_columns):
-            lo, hi = x_cuts[a][i], x_cuts[a][i + 1]
-            mid = lo + vector_columns
+        def by_offs(tile, lo, hi):
+            window = tile[:, 0 : window_columns(hi - lo)]
+            return window.indirect(offs_sb[:, lo // PER_COLUMN : hi // PER_COLUMN])
+
+        def interleave(a, i, vector_tokens):
+            lo, hi = X_CUTS[a][i], X_CUTS[a][i + 1]
+            mid = lo + vector_tokens
             if mid > lo:
-                dst, src = interleaved_views(xb[a][:, lo:mid, :], x_sb[a][i][:, :, 0 : mid - lo])
-                nc.vector.tensor_copy(dst, src)
-            if hi > mid:
-                c0, c1 = mid, hi
-                dst, src = interleaved_views(xb[a][:, c0:c1, :], x_sb[a][i][:, :, c0 - lo : c1 - lo])
-                nc.scalar.activation(dst, src, COPY)
+                nc.vector.tensor_copy(*interleaved_views(rounded[a][:, lo:mid, :], x_sb[a][i][:, :, 0 : mid - lo]))
+            dst, src = interleaved_views(rounded[a][:, mid:hi, :], x_sb[a][i][:, :, mid - lo : hi - lo])
+            nc.scalar.activation(dst, src, COPY)
 
-        def quantize(a, lo, hi):
-            nc.vector.quantize_mx(
-                out=words[a][:, lo:hi].bitcast(FP8X4),
-                scales=bytes3[4 * a :, lo:hi],
-                in_=xb[a][:, lo:hi, :].rearrange("p t j -> p (t j)"),
-            )
-
-        def slot_words(a, lo, hi):
-            if a == 1 and lo >= HELD:
-                return held[0][:, lo - HELD : hi - HELD]
-            return gwords[a][:, lo:hi]
+        def quantize(a, token_cuts):
+            for lo, hi in zip(token_cuts, token_cuts[1:]):
+                nc.vector.quantize_mx(
+                    out=token_words[a][:, lo:hi].bitcast(FP8X4),
+                    scales=token_scales[PLANE_STEP * a :, lo:hi],
+                    in_=rounded[a][:, lo:hi, :].rearrange("p t j -> p (t j)"),
+                )
 
         def gather_words(a, lo, hi):
-            nc.vector.tensor_copy(slot_words(a, lo, hi), words[a][:, 0 : window(hi - lo)].indirect(offs_sb[:, lo // 16 : hi // 16]))
+            nc.vector.tensor_copy(gathered(a, lo, hi), by_offs(token_words[a], lo, hi))
 
-        def gather_bytes(lo, hi):
-            nc.vector.tensor_copy(gbytes[0][:, lo:hi], bytes3[:, 0 : window(hi - lo)].indirect(offs_sb[:, lo // 16 : hi // 16]))
-
-        def shift_bytes(lo, hi, queue):
-            for a in (1, 2):
+        def gather_scales(lo, hi, queue):
+            nc.vector.tensor_copy(slot_scales[0][:, lo:hi], by_offs(token_scales, lo, hi))
+            for a in range(1, PASSES):
+                first_row = PLANE_STEP * a
                 queue.dma_start(
-                    out=gbytes[a][0:112, lo:hi].bitcast(I32), in_=gbytes[0][4 * a : 4 * a + 112, lo:hi].bitcast(I32)
+                    out=slot_scales[a][0:PLANE_ROWS, lo:hi].bitcast(I32),
+                    in_=slot_scales[0][first_row : first_row + PLANE_ROWS, lo:hi].bitcast(I32),
                 )
 
         acc = {}
@@ -134,74 +155,73 @@ def tile_moe_tk_lin_silu_kernel(
             cols = slice(e * C, (e + 1) * C)
             if a == 0:
                 acc[e] = psum.tile([P, C], F32, name="acc")
-            piece = max(j for j, e0 in enumerate(w_cuts) if e0 <= e)
-            i = e * A + a
+            load = max(i for i, e0 in enumerate(W_CUTS) if e0 <= e)
             nc.tensor.matmul_mx(
                 out=acc[e][:],
-                lhsT=w_sb[piece][:, i - w_cuts[piece] * A, :].bitcast(FP4X4),
-                lhsT_scale=ws_sb[:, i, :],
-                rhs=slot_words(a, e * C, (e + 1) * C).bitcast(FP8X4),
-                rhs_scale=gbytes[a][:, cols],
+                lhsT=w_sb[load][:, (e - W_CUTS[load]) * PASSES + a, :].bitcast(FP4X4),
+                lhsT_scale=w_planes[:, e * PASSES + a, :],
+                rhs=gathered(a, cols.start, cols.stop).bitcast(FP8X4),
+                rhs_scale=slot_scales[a][:, cols],
                 start=(a == 0),
-                stop=(a == A - 1),
+                stop=(a == PASSES - 1),
             )
-            if a == A - 1:
+            if a == PASSES - 1:
                 nc.scalar.activation(y_sb[:, cols], acc[e][:], SILU, bias=b_sb[:, e : e + 1])
                 if e + BANKS < E:
                     multiply(e + BANKS, 0)
 
-        interleave(0, 0, 256)
-        quantize(0, 0, 256)
-        interleave(0, 1, 176)
-        quantize(0, 256, 384)
-        quantize(0, 384, 640)
-        for i in range(2):
-            interleave(1, i, 0)
-        for i in range(2):
-            interleave(2, i, 0)
-        ws_rows = ws_sb[:].rearrange("p i n -> p (i n)").bitcast(I32)
+        def last_pass(expert_cuts):
+            for e0, e1 in zip(expert_cuts, expert_cuts[1:]):
+                gather_words(2, e0 * C, e1 * C)
+                for e in range(e0, e1):
+                    multiply(e, 2)
+
+        interleave(0, 0, VECTOR_TOKENS[0])
+        quantize(0, [0, 256])
+        interleave(0, 1, VECTOR_TOKENS[1])
+        quantize(0, [256, 384, T])
+        for a in range(1, PASSES):
+            for i in range(2):
+                interleave(a, i, 0)
         for r in range(1, 4):
-            nc.scalar.dma_start(out=ws_rows[r:P:32], in_=ws_rows[8 * r : P : 32])
-        gather_words(0, 0, 1536)
-        gather_words(0, 1536, S)
-        quantize(1, 0, 512)
-        quantize(1, 512, 640)
-        gather_words(1, 0, HELD)
-        quantize(2, 0, 512)
-        quantize(2, 512, 640)
-        held.append(keep.tile([P, S - HELD], U32, name="held", tag="xb2", align_bytes=64))
-        gather_bytes(0, 960)
-        shift_bytes(0, 960, nc.scalar)
-        gather_bytes(960, 1920)
-        shift_bytes(960, 1920, nc.sync)
+            nc.scalar.dma_start(out=w_plane_rows[r:P:32], in_=w_plane_rows[8 * r : P : 32])
+
+        gather_words(0, 0, S - C)
+        quantize(1, [0, 512, T])
+        apart[0, S - C] = keep.tile([P, C], U32, name="after_pass1", tag="x1_1", align_bytes=64)
+        gather_words(0, S - C, S)
+        gather_words(1, 0, HELD - C)
+        quantize(2, [0, 512, T])
+        apart[1, HELD - C] = keep.tile([P, C], U32, name="after_pass2", tag="x2_1", align_bytes=64)
+        gather_words(1, HELD - C, HELD)
+        apart[1, HELD] = keep.tile([P, S - HELD], U32, name="held", tag="rounded2", align_bytes=64)
+
+        gather_scales(0, S // 2, nc.scalar)
+        gather_scales(S // 2, S, nc.sync)
+
         for e in range(BANKS):
             multiply(e, 0)
-        for e in range(7):
+        for e in range(FIRST_HALF):
             multiply(e, 1)
-        for lo, hi in [(0, 384), (384, 896)]:
-            gather_words(2, lo, hi)
-            for e in range(lo // C, hi // C):
-                multiply(e, 2)
-        gather_words(2, 896, HELD)
+        last_pass([0, W_CUTS[1], FIRST_HALF])
+        gather_words(2, FIRST_HALF * C, HELD)
         for a in (1, 2):
-            for e in range(7, HELD // C):
+            for e in range(FIRST_HALF, HELD // C):
                 multiply(e, a)
         gather_words(1, HELD, S)
         for e in range(HELD // C, E):
             multiply(e, 1)
-        for lo, hi in [(HELD, 1664), (1664, 1792), (1792, S)]:
-            gather_words(2, lo, hi)
-            for e in range(lo // C, hi // C):
-                multiply(e, 2)
+        last_pass([HELD // C, E - 2, E - 1, E])
 
         gate_sb = keep.tile([P, TOP, T], F32, name="gate_sb", tag="w0", align_bytes=64)
         for r in range(TOP):
             nc.sync.dma_start(gate_sb[:, r, :], gate[r])
+
         for r in range(TOP):
             nc.vector.tensor_tensor(prod[r][:], y_sb[:].indirect(pos_sb[r][:]), gate_sb[:, r, :], MULT)
-        halves = (slice(0, 320), slice(320, 640))
-        for ts in halves:
-            nc.vector.tensor_tensor(part[:, ts], prod[0][:, ts], prod[1][:, ts], ADD)
-        for ts in halves:
-            nc.vector.tensor_tensor(o_sb[:, ts], part[:, ts], prod[2][:, ts], ADD)
-            nc.sync.dma_start(out[:, ts], o_sb[:, ts])
+        halves = (slice(0, T // 2), slice(T // 2, T))
+        for tokens in halves:
+            nc.vector.tensor_tensor(part[:, tokens], prod[0][:, tokens], prod[1][:, tokens], ADD)
+        for tokens in halves:
+            nc.vector.tensor_tensor(out_sb[:, tokens], part[:, tokens], prod[2][:, tokens], ADD)
+            nc.sync.dma_start(out[:, tokens], out_sb[:, tokens])

@@ -21,6 +21,8 @@ W_CUTS = [0, 3, BANKS, 13, E]
 HELD = 11 * C
 FIRST_HALF = (S // 2) // C
 
+OUT_CUTS = [0, 256, 512, T]
+
 F32 = mybir.dt.float32
 BF16 = mybir.dt.bfloat16
 U32 = mybir.dt.uint32
@@ -79,7 +81,8 @@ def tile_moe_tk_lin_silu_kernel(
         w_planes = keep.tile([P, E * PASSES, N], U8, name="w_planes", align_bytes=64)
         b_sb = keep.tile([P, E], F32, name="b_sb")
         y_sb = keep.tile([P, S], F32, name="y_sb")
-        prod = [keep.tile([P, T], F32, name=f"prod{r}") for r in range(TOP)]
+        picked = keep.tile([P, TOP, T], F32, name="picked")
+        prod = keep.tile([P, TOP, T], F32, name="prod")
         part = keep.tile([P, T], F32, name="part")
         out_sb = keep.tile([P, T], F32, name="out_sb")
 
@@ -217,11 +220,36 @@ def tile_moe_tk_lin_silu_kernel(
         for r in range(TOP):
             nc.sync.dma_start(gate_sb[:, r, :], gate[r])
 
-        for r in range(TOP):
-            nc.vector.tensor_tensor(prod[r][:], y_sb[:].indirect(pos_sb[r][:]), gate_sb[:, r, :], MULT)
-        halves = (slice(0, T // 2), slice(T // 2, T))
-        for tokens in halves:
-            nc.vector.tensor_tensor(part[:, tokens], prod[0][:, tokens], prod[1][:, tokens], ADD)
-        for tokens in halves:
-            nc.vector.tensor_tensor(out_sb[:, tokens], part[:, tokens], prod[2][:, tokens], ADD)
+        parts = [slice(lo, hi) for lo, hi in zip(OUT_CUTS, OUT_CUTS[1:])]
+
+        def by_pos(r, tokens):
+            return y_sb[:].indirect(pos_sb[r][:, tokens.start // PER_COLUMN : tokens.stop // PER_COLUMN])
+
+        def product(r0, r1, tokens):
+            nc.vector.tensor_tensor(prod[:, r0:r1, tokens], picked[:, r0:r1, tokens], gate_sb[:, r0:r1, tokens], MULT)
+
+        def first_sum(tokens):
+            nc.vector.tensor_tensor(part[:, tokens], prod[:, 0, tokens], prod[:, 1, tokens], ADD)
+
+        def second_sum(tokens):
+            nc.vector.tensor_tensor(out_sb[:, tokens], part[:, tokens], prod[:, 2, tokens], ADD)
             nc.sync.dma_start(out[:, tokens], out_sb[:, tokens])
+
+        for tokens in parts:
+            for r in range(0 if tokens == parts[-1] else 1, TOP):
+                nc.scalar.activation(picked[:, r, tokens], by_pos(r, tokens), COPY)
+        for tokens in parts[:-1]:
+            nc.vector.tensor_tensor(prod[:, 0, tokens], by_pos(0, tokens), gate_sb[:, 0, tokens], MULT)
+        a_part, b_part, c_part = parts
+        product(1, 2, a_part)
+        product(2, 3, a_part)
+        first_sum(a_part)
+        product(1, 2, b_part)
+        second_sum(a_part)
+        product(2, 3, b_part)
+        first_sum(b_part)
+        product(0, 2, c_part)
+        second_sum(b_part)
+        product(2, 3, c_part)
+        first_sum(c_part)
+        second_sum(c_part)

@@ -15,8 +15,8 @@ PER_COLUMN = 16
 PLANE_STEP = 4
 PLANE_ROWS = 100
 
-X_CUTS = [[0, 384, T], [0, 320, T], [0, 384, T]]
-VECTOR_TOKENS = (256, 176)
+X_CUTS = [[0, 256, 512, T], [0, 256, 512, T], [0, 384, T]]
+VECTOR_TOKENS = (192, 160, 80)
 W_CUTS = [0, 3, BANKS, 13, E]
 HELD = 11 * C
 FIRST_HALF = (S // 2) // C
@@ -179,19 +179,18 @@ def tile_moe_tk_lin_silu_kernel(
                 for e in range(e0, e1):
                     multiply(e, 2)
 
-        interleave(0, 0, VECTOR_TOKENS[0])
-        quantize(0, [0, 256])
-        interleave(0, 1, VECTOR_TOKENS[1])
-        quantize(0, [256, 384, T])
+        for i, vector_tokens in enumerate(VECTOR_TOKENS):
+            interleave(0, i, vector_tokens)
+            quantize(0, X_CUTS[0][i : i + 2])
         for a in range(1, PASSES):
-            for i in range(2):
+            for i in range(len(X_CUTS[a]) - 1):
                 interleave(a, i, 0)
         for r in range(1, 4):
             nc.scalar.dma_start(out=w_plane_rows[r:P:32], in_=w_plane_rows[8 * r : P : 32])
 
         gather_words(0, 0, S - C)
         quantize(1, [0, 512, T])
-        apart[0, S - C] = keep.tile([P, C], U32, name="after_pass1", tag="x1_1", align_bytes=64)
+        apart[0, S - C] = keep.tile([P, C], U32, name="after_pass1", tag="x1_2", align_bytes=64)
         gather_words(0, S - C, S)
         gather_words(1, 0, HELD - C)
         quantize(2, [0, 512, T])
@@ -238,8 +237,8 @@ def tile_moe_tk_lin_silu_kernel(
         for tokens in parts:
             for r in range(0 if tokens == parts[-1] else 1, TOP):
                 nc.scalar.activation(picked[:, r, tokens], by_pos(r, tokens), COPY)
-        for tokens in parts[:-1]:
-            nc.vector.tensor_tensor(prod[:, 0, tokens], by_pos(0, tokens), gate_sb[:, 0, tokens], MULT)
+        fused = slice(0, OUT_CUTS[-2])
+        nc.vector.tensor_tensor(prod[:, 0, fused], by_pos(0, fused), gate_sb[:, 0, fused], MULT)
         a_part, b_part, c_part = parts
         product(1, 2, a_part)
         product(2, 3, a_part)
@@ -249,7 +248,9 @@ def tile_moe_tk_lin_silu_kernel(
         product(2, 3, b_part)
         first_sum(b_part)
         product(0, 2, c_part)
-        second_sum(b_part)
+        b_middle = (b_part.start + b_part.stop) // 2
+        second_sum(slice(b_part.start, b_middle))
         product(2, 3, c_part)
         first_sum(c_part)
+        second_sum(slice(b_middle, b_part.stop))
         second_sum(c_part)

@@ -16,7 +16,7 @@ PLANE_STEP = 4
 PLANE_ROWS = 100
 
 X_CUTS = [[0, 256, 512, T], [0, 256, 512, T], [0, 384, T]]
-VECTOR_TOKENS = (192, 160, 80)
+VECTOR_TOKENS = (192, 128, 80)
 W_CUTS = [0, 3, BANKS, 13, E]
 HELD = 11 * C
 FIRST_HALF = (S // 2) // C
@@ -129,8 +129,9 @@ def tile_moe_tk_lin_silu_kernel(
             mid = lo + vector_tokens
             if mid > lo:
                 nc.vector.tensor_copy(*interleaved_views(rounded[a][:, lo:mid, :], x_sb[a][i][:, :, 0 : mid - lo]))
-            dst, src = interleaved_views(rounded[a][:, mid:hi, :], x_sb[a][i][:, :, mid - lo : hi - lo])
-            nc.scalar.activation(dst, src, COPY)
+            if hi > mid:
+                dst, src = interleaved_views(rounded[a][:, mid:hi, :], x_sb[a][i][:, :, mid - lo : hi - lo])
+                nc.scalar.activation(dst, src, COPY)
 
         def quantize(a, token_cuts):
             for lo, hi in zip(token_cuts, token_cuts[1:]):
@@ -179,9 +180,11 @@ def tile_moe_tk_lin_silu_kernel(
                 for e in range(e0, e1):
                     multiply(e, 2)
 
-        for i, vector_tokens in enumerate(VECTOR_TOKENS):
-            interleave(0, i, vector_tokens)
-            quantize(0, X_CUTS[0][i : i + 2])
+        interleave(0, 0, VECTOR_TOKENS[0])
+        quantize(0, X_CUTS[0][:2])
+        for i in (1, 2):
+            interleave(0, i, VECTOR_TOKENS[i])
+        quantize(0, X_CUTS[0][1:])
         for a in range(1, PASSES):
             for i in range(len(X_CUTS[a]) - 1):
                 interleave(a, i, 0)
@@ -216,8 +219,7 @@ def tile_moe_tk_lin_silu_kernel(
         last_pass([HELD // C, E - 2, E - 1, E])
 
         gate_sb = keep.tile([P, TOP, T], F32, name="gate_sb", tag="w0", align_bytes=64)
-        for r in range(TOP):
-            nc.sync.dma_start(gate_sb[:, r, :], gate[r])
+        nc.sync.dma_start(gate_sb[:], gate.rearrange("r n t -> n r t"))
 
         parts = [slice(lo, hi) for lo, hi in zip(OUT_CUTS, OUT_CUTS[1:])]
 

@@ -71,7 +71,7 @@ def tile_moe_tk_lin_silu_kernel(
             keep.tile([P, window_columns(S - C if a == 0 else HELD)], U32, name=f"token_words{a}", align_bytes=64)
             for a in range(PASSES)
         ]
-        token_scales = keep.tile([P, window_columns(S // 2)], U8, name="token_scales", align_bytes=64)
+        token_scales = keep.tile([P, window_columns(S // 2)], U8, name="token_scales", tag="token_scales", align_bytes=64)
         slot_words = [keep.tile([P, S], U32, name=f"slot_words{a}", align_bytes=64) for a in range(PASSES)]
         slot_scales = [keep.tile([P, S], U8, name=f"slot_scales{a}", align_bytes=64) for a in range(PASSES)]
         w_sb = [
@@ -204,6 +204,10 @@ def tile_moe_tk_lin_silu_kernel(
         gather_scales(0, S // 2, nc.scalar)
         gather_scales(S // 2, S, nc.sync)
 
+        gate_sb = keep.tile([P, TOP, T], F32, name="gate_sb", tag="token_scales", align_bytes=64)
+        for r in range(TOP):
+            nc.sync.dma_start(gate_sb[:, r, :], gate[r])
+
         for e in range(BANKS):
             multiply(e, 0)
         for e in range(FIRST_HALF):
@@ -217,9 +221,6 @@ def tile_moe_tk_lin_silu_kernel(
         for e in range(HELD // C, E):
             multiply(e, 1)
         last_pass([HELD // C, E - 2, E - 1, E])
-
-        gate_sb = keep.tile([P, TOP, T], F32, name="gate_sb", tag="w0", align_bytes=64)
-        nc.sync.dma_start(gate_sb[:], gate.rearrange("r n t -> n r t"))
 
         parts = [slice(lo, hi) for lo, hi in zip(OUT_CUTS, OUT_CUTS[1:])]
 

@@ -10,14 +10,15 @@ P = 128
 PACK = 4
 PASSES = K // (P * PACK)
 S = E * C
-BANKS = 8
+BANKS = 7
+LATE_BANKS = 4
 PER_COLUMN = 16
 PLANE_STEP = 4
 PLANE_ROWS = 100
 
 X_CUTS = [[0, 256, 512, T], [0, 256, 512, T], [0, 384, T]]
 VECTOR_TOKENS = (192, 128, 80)
-W_CUTS = [0, 3, BANKS, 13, E]
+W_CUTS = [0, 3, 8, 13, E]
 HELD = 11 * C
 FIRST_HALF = (S // 2) // C
 
@@ -53,7 +54,7 @@ def tile_moe_tk_lin_silu_kernel(
     nc = tc.nc
     with ExitStack() as ctx:
         keep = ctx.enter_context(tc.tile_pool(name="keep", bufs=1))
-        psum = ctx.enter_context(tc.psum_pool(name="psum", bufs=BANKS))
+        psum = ctx.enter_context(tc.psum_pool(name="psum", bufs=1))
 
         offs_sb = keep.tile([P, S // PER_COLUMN], U16, name="offs_sb")
         pos_sb = [keep.tile([P, T // PER_COLUMN], U16, name=f"pos{r}_sb") for r in range(TOP)]
@@ -158,7 +159,8 @@ def tile_moe_tk_lin_silu_kernel(
         def multiply(e, a):
             cols = slice(e * C, (e + 1) * C)
             if a == 0:
-                acc[e] = psum.tile([P, C], F32, name="acc")
+                bank = e if e < BANKS else (e - BANKS) % LATE_BANKS
+                acc[e] = psum.tile([P, C], F32, name=f"acc{e}", tag=f"bank{bank}")
             load = max(i for i, e0 in enumerate(W_CUTS) if e0 <= e)
             nc.tensor.matmul_mx(
                 out=acc[e][:],
@@ -171,7 +173,7 @@ def tile_moe_tk_lin_silu_kernel(
             )
             if a == PASSES - 1:
                 nc.scalar.activation(y_sb[:, cols], acc[e][:], SILU, bias=b_sb[:, e : e + 1])
-                if e + BANKS < E:
+                if e < LATE_BANKS:
                     multiply(e + BANKS, 0)
 
         def last_pass(expert_cuts):
@@ -214,11 +216,12 @@ def tile_moe_tk_lin_silu_kernel(
             multiply(e, 1)
         last_pass([0, W_CUTS[1], FIRST_HALF])
         gather_words(2, FIRST_HALF * C, HELD)
-        for a in (1, 2):
-            for e in range(FIRST_HALF, HELD // C):
+        for e in range(FIRST_HALF, HELD // C):
+            for a in (1, 2):
                 multiply(e, a)
         gather_words(1, HELD, S)
         for e in range(HELD // C, E):
+            multiply(e, 0)
             multiply(e, 1)
         last_pass([HELD // C, E - 2, E - 1, E])
 

@@ -22,7 +22,8 @@ W_CUTS = [0, 3, 8, 13, E]
 HELD = 11 * C
 FIRST_HALF = (S // 2) // C
 
-OUT_CUTS = [0, 256, 512, T]
+SECOND_CUTS = [0, 384, T]
+THIRD_CUTS = [0, 256, 512, T]
 
 F32 = mybir.dt.float32
 BF16 = mybir.dt.bfloat16
@@ -82,7 +83,7 @@ def tile_moe_tk_lin_silu_kernel(
         w_planes = keep.tile([P, E * PASSES, N], U8, name="w_planes", align_bytes=64)
         b_sb = keep.tile([P, E], F32, name="b_sb")
         y_sb = keep.tile([P, S], F32, name="y_sb")
-        picked = keep.tile([P, TOP, T], F32, name="picked")
+        picked = keep.tile([P, TOP - 1, T], F32, name="picked")
         prod = keep.tile([P, TOP, T], F32, name="prod")
         part = keep.tile([P, T], F32, name="part")
         out_sb = keep.tile([P, T], F32, name="out_sb")
@@ -225,13 +226,11 @@ def tile_moe_tk_lin_silu_kernel(
             multiply(e, 1)
         last_pass([HELD // C, E - 2, E - 1, E])
 
-        parts = [slice(lo, hi) for lo, hi in zip(OUT_CUTS, OUT_CUTS[1:])]
-
         def by_pos(r, tokens):
             return y_sb[:].indirect(pos_sb[r][:, tokens.start // PER_COLUMN : tokens.stop // PER_COLUMN])
 
-        def product(r0, r1, tokens):
-            nc.vector.tensor_tensor(prod[:, r0:r1, tokens], picked[:, r0:r1, tokens], gate_sb[:, r0:r1, tokens], MULT)
+        def product(r, tokens):
+            nc.vector.tensor_tensor(prod[:, r, tokens], picked[:, r - 1, tokens], gate_sb[:, r, tokens], MULT)
 
         def first_sum(tokens):
             nc.vector.tensor_tensor(part[:, tokens], prod[:, 0, tokens], prod[:, 1, tokens], ADD)
@@ -240,23 +239,18 @@ def tile_moe_tk_lin_silu_kernel(
             nc.vector.tensor_tensor(out_sb[:, tokens], part[:, tokens], prod[:, 2, tokens], ADD)
             nc.sync.dma_start(out[:, tokens], out_sb[:, tokens])
 
-        for tokens in parts:
-            for r in range(0 if tokens == parts[-1] else 1, TOP):
-                nc.scalar.activation(picked[:, r, tokens], by_pos(r, tokens), COPY)
-        fused = slice(0, OUT_CUTS[-2])
-        nc.vector.tensor_tensor(prod[:, 0, fused], by_pos(0, fused), gate_sb[:, 0, fused], MULT)
-        a_part, b_part, c_part = parts
-        product(1, 2, a_part)
-        product(2, 3, a_part)
-        first_sum(a_part)
-        product(1, 2, b_part)
-        second_sum(a_part)
-        product(2, 3, b_part)
-        first_sum(b_part)
-        product(0, 2, c_part)
-        b_middle = (b_part.start + b_part.stop) // 2
-        second_sum(slice(b_part.start, b_middle))
-        product(2, 3, c_part)
-        first_sum(c_part)
-        second_sum(slice(b_middle, b_part.stop))
-        second_sum(c_part)
+        second = [slice(lo, hi) for lo, hi in zip(SECOND_CUTS, SECOND_CUTS[1:])]
+        third = [slice(lo, hi) for lo, hi in zip(THIRD_CUTS, THIRD_CUTS[1:])]
+        for r, parts in ((1, second), (2, third)):
+            for tokens in parts:
+                nc.scalar.activation(picked[:, r - 1, tokens], by_pos(r, tokens), COPY)
+        nc.vector.tensor_tensor(prod[:, 0, :], by_pos(0, slice(0, T)), gate_sb[:, 0, :], MULT)
+        for tokens in second:
+            product(1, tokens)
+        first_sum(second[0])
+        product(2, third[0])
+        first_sum(second[1])
+        for done, tokens in zip(third, third[1:]):
+            product(2, tokens)
+            second_sum(done)
+        second_sum(third[-1])

@@ -13,6 +13,7 @@ S = E * C
 BANKS = 7
 LATE_BANKS = 4
 PER_COLUMN = 16
+ALIGN = 256
 PLANE_STEP = 4
 PLANE_ROWS = 100
 
@@ -61,32 +62,32 @@ def tile_moe_tk_lin_silu_kernel(
         pos_sb = [keep.tile([P, T // PER_COLUMN], U16, name=f"pos{r}_sb") for r in range(TOP)]
         x_sb = [
             [
-                keep.tile([P, PACK, hi - lo], F32, name=f"x{a}_{i}", tag=f"x{a}_{i}", align_bytes=64)
+                keep.tile([P, PACK, hi - lo], F32, name=f"x{a}_{i}", tag=f"x{a}_{i}", align_bytes=ALIGN)
                 for i, (lo, hi) in enumerate(zip(X_CUTS[a], X_CUTS[a][1:]))
             ]
             for a in range(PASSES)
         ]
         rounded = [
-            keep.tile([P, T, PACK], BF16, name=f"rounded{a}", tag=f"rounded{a}", align_bytes=64) for a in range(PASSES)
+            keep.tile([P, T, PACK], BF16, name=f"rounded{a}", tag=f"rounded{a}", align_bytes=ALIGN) for a in range(PASSES)
         ]
         token_words = [
-            keep.tile([P, window_columns(S - C if a == 0 else HELD)], U32, name=f"token_words{a}", align_bytes=64)
+            keep.tile([P, window_columns(S - C if a == 0 else HELD)], U32, name=f"token_words{a}", align_bytes=ALIGN)
             for a in range(PASSES)
         ]
-        token_scales = keep.tile([P, window_columns(S // 2)], U8, name="token_scales", tag="token_scales", align_bytes=64)
-        slot_words = [keep.tile([P, S], U32, name=f"slot_words{a}", align_bytes=64) for a in range(PASSES)]
-        slot_scales = [keep.tile([P, S], U8, name=f"slot_scales{a}", align_bytes=64) for a in range(PASSES)]
+        token_scales = keep.tile([P, window_columns(S // 2)], U8, name="token_scales", tag="token_scales", align_bytes=ALIGN)
+        slot_words = [keep.tile([P, S], U32, name=f"slot_words{a}", align_bytes=ALIGN) for a in range(PASSES)]
+        slot_scales = [keep.tile([P, S], U8, name=f"slot_scales{a}", align_bytes=ALIGN) for a in range(PASSES)]
         w_sb = [
-            keep.tile([P, (e1 - e0) * PASSES, 2 * N], U8, name=f"w{e0}", tag=f"w{e0}", align_bytes=64)
+            keep.tile([P, (e1 - e0) * PASSES, 2 * N], U8, name=f"w{e0}", tag=f"w{e0}", align_bytes=ALIGN)
             for e0, e1 in zip(W_CUTS, W_CUTS[1:])
         ]
-        w_planes = keep.tile([P, E * PASSES, N], U8, name="w_planes", align_bytes=64)
+        w_planes = keep.tile([P, E * PASSES, N], U8, name="w_planes", align_bytes=ALIGN)
         b_sb = keep.tile([P, E], F32, name="b_sb")
-        y_sb = keep.tile([P, S], F32, name="y_sb")
-        picked = keep.tile([P, TOP - 1, T], F32, name="picked")
-        prod = keep.tile([P, TOP, T], F32, name="prod")
-        part = keep.tile([P, T], F32, name="part")
-        out_sb = keep.tile([P, T], F32, name="out_sb")
+        y_sb = keep.tile([P, S], F32, name="y_sb", align_bytes=ALIGN)
+        picked = keep.tile([P, TOP - 1, T], F32, name="picked", align_bytes=ALIGN)
+        prod = keep.tile([P, TOP, T], F32, name="prod", align_bytes=ALIGN)
+        part = keep.tile([P, T], F32, name="part", align_bytes=ALIGN)
+        out_sb = keep.tile([P, T], F32, name="out_sb", align_bytes=ALIGN)
 
         w_plane_rows = w_planes[:].rearrange("p i n -> p (i n)").bitcast(I32)
         nc.vector.memset(w_plane_rows, 0)
@@ -196,18 +197,18 @@ def tile_moe_tk_lin_silu_kernel(
 
         gather_words(0, 0, S - C)
         quantize(1, [0, 512, T])
-        apart[0, S - C] = keep.tile([P, C], U32, name="after_pass1", tag="x1_2", align_bytes=64)
+        apart[0, S - C] = keep.tile([P, C], U32, name="after_pass1", tag="x1_2", align_bytes=ALIGN)
         gather_words(0, S - C, S)
         gather_words(1, 0, HELD - C)
         quantize(2, [0, 512, T])
-        apart[1, HELD - C] = keep.tile([P, C], U32, name="after_pass2", tag="x2_1", align_bytes=64)
+        apart[1, HELD - C] = keep.tile([P, C], U32, name="after_pass2", tag="x2_1", align_bytes=ALIGN)
         gather_words(1, HELD - C, HELD)
-        apart[1, HELD] = keep.tile([P, S - HELD], U32, name="held", tag="rounded2", align_bytes=64)
+        apart[1, HELD] = keep.tile([P, S - HELD], U32, name="held", tag="rounded2", align_bytes=ALIGN)
 
         gather_scales(0, S // 2, nc.scalar)
         gather_scales(S // 2, S, nc.sync)
 
-        gate_sb = keep.tile([P, TOP, T], F32, name="gate_sb", tag="token_scales", align_bytes=64)
+        gate_sb = keep.tile([P, TOP, T], F32, name="gate_sb", tag="token_scales", align_bytes=ALIGN)
         for r in range(TOP):
             nc.sync.dma_start(gate_sb[:, r, :], gate[r])
 

@@ -18,10 +18,10 @@ PLANE_STEP = 4
 PLANE_ROWS = 100
 
 X_CUTS = [[0, 256, 512, T], [0, 256, 512, T], [0, 384, T]]
-VECTOR_TOKENS = (192, 128, 80)
+VECTOR_TOKENS = (192, 160, 80)
 W_CUTS = [0, 3, 8, 13, E]
 HELD = 11 * C
-FIRST_HALF = (S // 2) // C
+FIRST_HALF = BANKS
 
 SECOND_CUTS = [0, 384, T]
 THIRD_CUTS = [0, 256, 512, T]
@@ -205,8 +205,8 @@ def tile_moe_tk_lin_silu_kernel(
         gather_words(1, HELD - C, HELD)
         apart[1, HELD] = keep.tile([P, S - HELD], U32, name="held", tag="rounded2", align_bytes=ALIGN)
 
-        gather_scales(0, S // 2, nc.scalar)
-        gather_scales(S // 2, S, nc.sync)
+        gather_scales(0, FIRST_HALF * C, nc.scalar)
+        gather_scales(FIRST_HALF * C, S, nc.sync)
 
         gate_sb = keep.tile([P, TOP, T], F32, name="gate_sb", tag="token_scales", align_bytes=ALIGN)
         for r in range(TOP):

@@ -13,7 +13,7 @@ S = E * C
 BANKS = 7
 LATE_BANKS = 4
 PER_COLUMN = 16
-ALIGN = 256
+ALIGN = 512
 PLANE_STEP = 4
 PLANE_ROWS = 100
 
@@ -108,12 +108,14 @@ def tile_moe_tk_lin_silu_kernel(
                 nc.sync.dma_start(offs_sb[:], offs)
         nc.sync.dma_start(b_sb[:], b)
         for i, (e0, e1) in enumerate(zip(W_CUTS, W_CUTS[1:])):
+            if e0 == W_CUTS[2]:
+                nc.sync.dma_start(pos_sb[0][:], pos1)
+                nc.sync.dma_start(pos_sb[1][:], pos2)
             nc.sync.dma_start(
                 out=w_sb[i][:].bitcast(I32),
                 in_=w_words[e0:e1].rearrange("e a p c -> p (e a) c").bitcast(I32),
             )
-        for r, positions in enumerate((pos1, pos2, pos3)):
-            nc.sync.dma_start(pos_sb[r][:], positions)
+        nc.sync.dma_start(pos_sb[2][:], pos3)
 
         apart = {}
 

@@ -11,7 +11,6 @@ PACK = 4
 PASSES = K // (P * PACK)
 S = E * C
 BANKS = 7
-LATE_BANKS = 4
 PER_COLUMN = 16
 ALIGN = 512
 PLANE_STEP = 4
@@ -149,9 +148,9 @@ def tile_moe_tk_lin_silu_kernel(
         def gather_words(a, lo, hi):
             nc.vector.tensor_copy(gathered(a, lo, hi), by_offs(token_words[a], lo, hi))
 
-        def gather_scales(lo, hi, queue):
+        def gather_scales(lo, hi, queue, passes):
             nc.vector.tensor_copy(slot_scales[0][:, lo:hi], by_offs(token_scales, lo, hi))
-            for a in range(1, PASSES):
+            for a in passes:
                 first_row = PLANE_STEP * a
                 queue.dma_start(
                     out=slot_scales[a][0:PLANE_ROWS, lo:hi].bitcast(I32),
@@ -163,7 +162,7 @@ def tile_moe_tk_lin_silu_kernel(
         def multiply(e, a):
             cols = slice(e * C, (e + 1) * C)
             if a == 0:
-                bank = e if e < BANKS else (e - BANKS) % LATE_BANKS
+                bank = e if e < BANKS else e - BANKS
                 acc[e] = psum.tile([P, C], F32, name=f"acc{e}", tag=f"bank{bank}")
             load = max(i for i, e0 in enumerate(W_CUTS) if e0 <= e)
             nc.tensor.matmul_mx(
@@ -177,7 +176,7 @@ def tile_moe_tk_lin_silu_kernel(
             )
             if a == PASSES - 1:
                 nc.scalar.activation(y_sb[:, cols], acc[e][:], SILU, bias=b_sb[:, e : e + 1])
-                if e < LATE_BANKS:
+                if e + BANKS < HELD // C:
                     multiply(e + BANKS, 0)
 
         def last_pass(expert_cuts):
@@ -207,8 +206,8 @@ def tile_moe_tk_lin_silu_kernel(
         gather_words(1, HELD - C, HELD)
         apart[1, HELD] = keep.tile([P, S - HELD], U32, name="held", tag="rounded2", align_bytes=ALIGN)
 
-        gather_scales(0, FIRST_HALF * C, nc.scalar)
-        gather_scales(FIRST_HALF * C, S, nc.sync)
+        gather_scales(0, FIRST_HALF * C, nc.scalar, (1, 2))
+        gather_scales(FIRST_HALF * C, S, nc.sync, (2, 1))
 
         gate_sb = keep.tile([P, TOP, T], F32, name="gate_sb", tag="token_scales", align_bytes=ALIGN)
         for r in range(TOP):
@@ -219,15 +218,18 @@ def tile_moe_tk_lin_silu_kernel(
         for e in range(FIRST_HALF):
             multiply(e, 1)
         last_pass([0, W_CUTS[1], FIRST_HALF])
-        gather_words(2, FIRST_HALF * C, HELD)
+        gather_words(2, FIRST_HALF * C, HELD + C)
         for e in range(FIRST_HALF, HELD // C):
             for a in (1, 2):
                 multiply(e, a)
-        gather_words(1, HELD, S)
         for e in range(HELD // C, E):
             multiply(e, 0)
-            multiply(e, 1)
-        last_pass([HELD // C, E - 2, E - 1, E])
+        gather_words(1, HELD, S)
+        for e in range(HELD // C, E):
+            if e > HELD // C:
+                gather_words(2, e * C, (e + 1) * C)
+            for a in (1, 2):
+                multiply(e, a)
 
         def by_pos(r, tokens):
             return y_sb[:].indirect(pos_sb[r][:, tokens.start // PER_COLUMN : tokens.stop // PER_COLUMN])

@@ -17,6 +17,7 @@ PLANE_STEP = 4
 PLANE_ROWS = 100
 
 X_CUTS = [[0, 256, 512, T], [0, 256, 512, T], [0, 384, T]]
+HEAD = X_CUTS[0][2]
 VECTOR_TOKENS = (192, 160, 80)
 W_CUTS = [0, 3, 8, 13, E]
 HELD = 11 * C
@@ -59,9 +60,12 @@ def tile_moe_tk_lin_silu_kernel(
 
         offs_sb = keep.tile([P, S // PER_COLUMN], U16, name="offs_sb")
         pos_sb = [keep.tile([P, T // PER_COLUMN], U16, name=f"pos{r}_sb") for r in range(TOP)]
+        x_head = keep.tile([P, PACK, HEAD], F32, name="x_head", align_bytes=ALIGN)
         x_sb = [
             [
-                keep.tile([P, PACK, hi - lo], F32, name=f"x{a}_{i}", tag=f"x{a}_{i}", align_bytes=ALIGN)
+                x_head[:, :, lo:hi]
+                if a == 0 and hi <= HEAD
+                else keep.tile([P, PACK, hi - lo], F32, name=f"x{a}_{i}", tag=f"x{a}_{i}", align_bytes=ALIGN)
                 for i, (lo, hi) in enumerate(zip(X_CUTS[a], X_CUTS[a][1:]))
             ]
             for a in range(PASSES)
@@ -96,8 +100,11 @@ def tile_moe_tk_lin_silu_kernel(
 
         for a in range(PASSES):
             rows = xT[a * P * PACK : (a + 1) * P * PACK, :].rearrange("(p j) t -> p j t", j=PACK)
+            if a == 0:
+                nc.sync.dma_start(out=x_head[:, 0, :], in_=rows[:, 0, 0:HEAD])
             for i, (lo, hi) in enumerate(zip(X_CUTS[a], X_CUTS[a][1:])):
-                nc.sync.dma_start(out=x_sb[a][i][:], in_=rows[:, :, lo:hi])
+                first_row = 1 if a == 0 and hi <= HEAD else 0
+                nc.sync.dma_start(out=x_sb[a][i][:, first_row:, :], in_=rows[:, first_row:, lo:hi])
                 if (a, i) == (PASSES - 1, 0):
                     nc.sync.dma_start(
                         out=w_planes[0:P:8].bitcast(I32),
@@ -134,8 +141,9 @@ def tile_moe_tk_lin_silu_kernel(
             if mid > lo:
                 nc.vector.tensor_copy(*interleaved_views(rounded[a][:, lo:mid, :], x_sb[a][i][:, :, 0 : mid - lo]))
             if hi > mid:
-                dst, src = interleaved_views(rounded[a][:, mid:hi, :], x_sb[a][i][:, :, mid - lo : hi - lo])
-                nc.scalar.activation(dst, src, COPY)
+                for rows in (slice(0, 1), slice(1, PACK)) if (a, i) == (0, 0) else (slice(0, PACK),):
+                    dst, src = interleaved_views(rounded[a][:, mid:hi, rows], x_sb[a][i][:, rows, mid - lo : hi - lo])
+                    nc.scalar.activation(dst, src, COPY)
 
         def quantize(a, token_cuts):
             for lo, hi in zip(token_cuts, token_cuts[1:]):

@@ -18,6 +18,7 @@ PLANE_ROWS = 100
 
 X_CUTS = [[0, 256, 512, T], [0, 256, 512, T], [0, 384, T]]
 HEAD = X_CUTS[0][2]
+WIDE = 512
 VECTOR_TOKENS = (192, 160, 80)
 W_CUTS = [0, 3, 8, 13, E]
 HELD = 11 * C
@@ -56,6 +57,7 @@ def tile_moe_tk_lin_silu_kernel(
     nc = tc.nc
     with ExitStack() as ctx:
         keep = ctx.enter_context(tc.tile_pool(name="keep", bufs=1))
+        late = ctx.enter_context(tc.tile_pool(name="late", bufs=1))
         psum = ctx.enter_context(tc.psum_pool(name="psum", bufs=1))
 
         offs_sb = keep.tile([P, S // PER_COLUMN], U16, name="offs_sb")
@@ -77,12 +79,12 @@ def tile_moe_tk_lin_silu_kernel(
             keep.tile([P, window_columns(S - C if a == 0 else HELD)], U32, name=f"token_words{a}", align_bytes=ALIGN)
             for a in range(PASSES)
         ]
-        token_scales = keep.tile([P, window_columns(S // 2)], U8, name="token_scales", tag="token_scales", align_bytes=ALIGN)
+        token_scales = late.tile([P, window_columns(S // 2)], U8, name="token_scales", align_bytes=ALIGN, offset=0)
         slot_words = [keep.tile([P, S], U32, name=f"slot_words{a}", align_bytes=ALIGN) for a in range(PASSES)]
         slot_scales = [keep.tile([P, S], U8, name=f"slot_scales{a}", align_bytes=ALIGN) for a in range(PASSES)]
         w_sb = [
             keep.tile([P, (e1 - e0) * PASSES, 2 * N], U8, name=f"w{e0}", tag=f"w{e0}", align_bytes=ALIGN)
-            for e0, e1 in zip(W_CUTS, W_CUTS[1:])
+            for e0, e1 in zip(W_CUTS, W_CUTS[1:-1])
         ]
         w_planes = keep.tile([P, E * PASSES, N], U8, name="w_planes", align_bytes=ALIGN)
         b_sb = keep.tile([P, E], F32, name="b_sb")
@@ -113,14 +115,16 @@ def tile_moe_tk_lin_silu_kernel(
             if a == 0:
                 nc.sync.dma_start(offs_sb[:], offs)
         nc.sync.dma_start(b_sb[:], b)
-        for i, (e0, e1) in enumerate(zip(W_CUTS, W_CUTS[1:])):
-            if e0 == W_CUTS[2]:
-                nc.sync.dma_start(pos_sb[0][:], pos1)
-                nc.sync.dma_start(pos_sb[1][:], pos2)
-            nc.sync.dma_start(
-                out=w_sb[i][:].bitcast(I32),
-                in_=w_words[e0:e1].rearrange("e a p c -> p (e a) c").bitcast(I32),
-            )
+
+        def load_weights(i):
+            rows = w_words[W_CUTS[i] : W_CUTS[i + 1]].rearrange("e a p c -> p (e a) c")
+            nc.sync.dma_start(out=w_sb[i][:].bitcast(I32), in_=rows.bitcast(I32))
+
+        load_weights(0)
+        load_weights(1)
+        nc.sync.dma_start(pos_sb[0][:], pos1)
+        load_weights(2)
+        nc.sync.dma_start(pos_sb[1][:], pos2)
         nc.sync.dma_start(pos_sb[2][:], pos3)
 
         apart = {}
@@ -140,9 +144,10 @@ def tile_moe_tk_lin_silu_kernel(
             mid = lo + vector_tokens
             if mid > lo:
                 nc.vector.tensor_copy(*interleaved_views(rounded[a][:, lo:mid, :], x_sb[a][i][:, :, 0 : mid - lo]))
-            if hi > mid:
+            cuts = [mid, WIDE, hi] if mid < WIDE < hi else [mid, hi]
+            for t0, t1 in zip(cuts, cuts[1:]):
                 for rows in (slice(0, 1), slice(1, PACK)) if (a, i) == (0, 0) else (slice(0, PACK),):
-                    dst, src = interleaved_views(rounded[a][:, mid:hi, rows], x_sb[a][i][:, rows, mid - lo : hi - lo])
+                    dst, src = interleaved_views(rounded[a][:, t0:t1, rows], x_sb[a][i][:, rows, t0 - lo : t1 - lo])
                     nc.scalar.activation(dst, src, COPY)
 
         def quantize(a, token_cuts):
@@ -205,11 +210,11 @@ def tile_moe_tk_lin_silu_kernel(
             nc.scalar.dma_start(out=w_plane_rows[r:P:32], in_=w_plane_rows[8 * r : P : 32])
 
         gather_words(0, 0, S - C)
-        quantize(1, [0, 512, T])
+        quantize(1, [0, WIDE, T])
         apart[0, S - C] = keep.tile([P, C], U32, name="after_pass1", tag="x1_2", align_bytes=ALIGN)
         gather_words(0, S - C, S)
         gather_words(1, 0, HELD - C)
-        quantize(2, [0, 512, T])
+        quantize(2, [0, WIDE, T])
         apart[1, HELD - C] = keep.tile([P, C], U32, name="after_pass2", tag="x2_1", align_bytes=ALIGN)
         gather_words(1, HELD - C, HELD)
         apart[1, HELD] = keep.tile([P, S - HELD], U32, name="held", tag="rounded2", align_bytes=ALIGN)
@@ -217,7 +222,10 @@ def tile_moe_tk_lin_silu_kernel(
         gather_scales(0, FIRST_HALF * C, nc.scalar, (1, 2))
         gather_scales(FIRST_HALF * C, S, nc.sync, (2, 1))
 
-        gate_sb = keep.tile([P, TOP, T], F32, name="gate_sb", tag="token_scales", align_bytes=ALIGN)
+        last_rows = (E - W_CUTS[-2]) * PASSES
+        w_sb.append(late.tile([P, last_rows, 2 * N], U8, name="w_last", align_bytes=ALIGN, offset=0))
+        load_weights(len(w_sb) - 1)
+        gate_sb = late.tile([P, TOP, T], F32, name="gate_sb", align_bytes=ALIGN, offset=last_rows * 2 * N)
         for r in range(TOP):
             nc.sync.dma_start(gate_sb[:, r, :], gate[r])
 

@@ -139,16 +139,16 @@ def tile_moe_tk_lin_silu_kernel(
             window = tile[:, 0 : window_columns(hi - lo)]
             return window.indirect(offs_sb[:, lo // PER_COLUMN : hi // PER_COLUMN])
 
-        def interleave(a, i, vector_tokens):
+        def interleave(a, i, vector_tokens, rows):
             lo, hi = X_CUTS[a][i], X_CUTS[a][i + 1]
             mid = lo + vector_tokens
             if mid > lo:
-                nc.vector.tensor_copy(*interleaved_views(rounded[a][:, lo:mid, :], x_sb[a][i][:, :, 0 : mid - lo]))
+                dst, src = interleaved_views(rounded[a][:, lo:mid, rows], x_sb[a][i][:, rows, 0 : mid - lo])
+                nc.vector.tensor_copy(dst, src)
             cuts = [mid, WIDE, hi] if mid < WIDE < hi else [mid, hi]
             for t0, t1 in zip(cuts, cuts[1:]):
-                for rows in (slice(0, 1), slice(1, PACK)) if (a, i) == (0, 0) else (slice(0, PACK),):
-                    dst, src = interleaved_views(rounded[a][:, t0:t1, rows], x_sb[a][i][:, rows, t0 - lo : t1 - lo])
-                    nc.scalar.activation(dst, src, COPY)
+                dst, src = interleaved_views(rounded[a][:, t0:t1, rows], x_sb[a][i][:, rows, t0 - lo : t1 - lo])
+                nc.scalar.activation(dst, src, COPY)
 
         def quantize(a, token_cuts):
             for lo, hi in zip(token_cuts, token_cuts[1:]):
@@ -198,14 +198,17 @@ def tile_moe_tk_lin_silu_kernel(
                 for e in range(e0, e1):
                     multiply(e, 2)
 
-        interleave(0, 0, VECTOR_TOKENS[0])
+        first_row, other_rows, all_rows = slice(0, 1), slice(1, PACK), slice(0, PACK)
+        for i in (0, 1):
+            interleave(0, i, VECTOR_TOKENS[i], first_row)
+        interleave(0, 0, VECTOR_TOKENS[0], other_rows)
         quantize(0, X_CUTS[0][:2])
-        for i in (1, 2):
-            interleave(0, i, VECTOR_TOKENS[i])
+        interleave(0, 1, VECTOR_TOKENS[1], other_rows)
+        interleave(0, 2, VECTOR_TOKENS[2], all_rows)
         quantize(0, X_CUTS[0][1:])
         for a in range(1, PASSES):
             for i in range(len(X_CUTS[a]) - 1):
-                interleave(a, i, 0)
+                interleave(a, i, 0, all_rows)
         for r in range(1, 4):
             nc.scalar.dma_start(out=w_plane_rows[r:P:32], in_=w_plane_rows[8 * r : P : 32])
 

from contextlib import ExitStack

import concourse.mybir as mybir

K, T, E, C, N = 1536, 640, 15, 128, 128
TOP = 3
FLOPS = 2 * K * N * E * C

P = 128
PACK = 4
PASSES = K // (P * PACK)
S = E * C
BANKS = 7
PER_COLUMN = 16
ALIGN = 512
PLANE_STEP = 4
PLANE_ROWS = 100

X_CUTS = [[0, 256, 512, T], [0, 256, 512, T], [0, 384, T]]
HEAD = X_CUTS[0][2]
WIDE = 512
VECTOR_TOKENS = (192, 160, 80)
W_CUTS = [0, 3, 8, 13, E]
HELD = 11 * C
FIRST_HALF = BANKS

SECOND_CUTS = [0, 384, T]
THIRD_CUTS = [0, 256, 512, T]

F32 = mybir.dt.float32
BF16 = mybir.dt.bfloat16
U32 = mybir.dt.uint32
I32 = mybir.dt.int32
U16 = mybir.dt.uint16
U8 = mybir.dt.uint8
FP8X4 = mybir.dt.float8_e4m3fn_x4
FP4X4 = mybir.dt.float4_e2m1fn_x4
COPY = mybir.ActivationFunctionType.Copy
SILU = mybir.ActivationFunctionType.Silu
ADD = mybir.AluOpType.add
MULT = mybir.AluOpType.mult


def interleaved_views(dst, src):
    return dst.rearrange("p (c i) j -> p c j i", i=4), src.rearrange("p j (c i) -> p c j i", i=4)


def window_columns(offsets):
    if offsets > 1536:
        return 4096
    return 2048 if offsets >= 256 else T


def tile_moe_tk_lin_silu_kernel(
    tc, xT, w_words, w_scales, b, gate, offs, pos1, pos2, pos3, out
):
    nc = tc.nc
    with ExitStack() as ctx:
        keep = ctx.enter_context(tc.tile_pool(name="keep", bufs=1))
        late = ctx.enter_context(tc.tile_pool(name="late", bufs=1))
        psum = ctx.enter_context(tc.psum_pool(name="psum", bufs=1))

        offs_sb = keep.tile([P, S // PER_COLUMN], U16, name="offs_sb")
        pos_sb = [keep.tile([P, T // PER_COLUMN], U16, name=f"pos{r}_sb") for r in range(TOP)]
        x_head = keep.tile([P, PACK, HEAD], F32, name="x_head", align_bytes=ALIGN)
        x_sb = [
            [
                x_head[:, :, lo:hi]
                if a == 0 and hi <= HEAD
                else keep.tile([P, PACK, hi - lo], F32, name=f"x{a}_{i}", tag=f"x{a}_{i}", align_bytes=ALIGN)
                for i, (lo, hi) in enumerate(zip(X_CUTS[a], X_CUTS[a][1:]))
            ]
            for a in range(PASSES)
        ]
        rounded = [
            keep.tile([P, T, PACK], BF16, name=f"rounded{a}", tag=f"rounded{a}", align_bytes=ALIGN) for a in range(PASSES)
        ]
        token_words = [
            keep.tile([P, window_columns(S - C if a == 0 else HELD)], U32, name=f"token_words{a}", align_bytes=ALIGN)
            for a in range(PASSES)
        ]
        token_scales = late.tile([P, window_columns(S // 2)], U8, name="token_scales", align_bytes=ALIGN, offset=0)
        slot_words = [keep.tile([P, S], U32, name=f"slot_words{a}", align_bytes=ALIGN) for a in range(PASSES)]
        slot_scales = [keep.tile([P, S], U8, name=f"slot_scales{a}", align_bytes=ALIGN) for a in range(PASSES)]
        w_sb = [
            keep.tile([P, (e1 - e0) * PASSES, 2 * N], U8, name=f"w{e0}", tag=f"w{e0}", align_bytes=ALIGN)
            for e0, e1 in zip(W_CUTS, W_CUTS[1:-1])
        ]
        w_planes = keep.tile([P, E * PASSES, N], U8, name="w_planes", align_bytes=ALIGN)
        b_sb = keep.tile([P, E], F32, name="b_sb")
        y_sb = keep.tile([P, S], F32, name="y_sb", align_bytes=ALIGN)
        picked = keep.tile([P, TOP - 1, T], F32, name="picked", align_bytes=ALIGN)
        prod = keep.tile([P, TOP, T], F32, name="prod", align_bytes=ALIGN)
        part = keep.tile([P, T], F32, name="part", align_bytes=ALIGN)
        out_sb = keep.tile([P, T], F32, name="out_sb", align_bytes=ALIGN)

        w_plane_rows = w_planes[:].rearrange("p i n -> p (i n)").bitcast(I32)
        nc.vector.memset(w_plane_rows, 0)
        nc.vector.memset(token_scales[:, 0:T].bitcast(I32), 0)
        for a in range(1, PASSES):
            nc.vector.memset(slot_scales[a][:].bitcast(I32), 0)

        for a in range(PASSES):
            rows = xT[a * P * PACK : (a + 1) * P * PACK, :].rearrange("(p j) t -> p j t", j=PACK)
            if a == 0:
                nc.sync.dma_start(out=x_head[:, 0, :], in_=rows[:, 0, 0:HEAD])
            for i, (lo, hi) in enumerate(zip(X_CUTS[a], X_CUTS[a][1:])):
                first_row = 1 if a == 0 and hi <= HEAD else 0
                nc.sync.dma_start(out=x_sb[a][i][:, first_row:, :], in_=rows[:, first_row:, lo:hi])
                if (a, i) == (PASSES - 1, 0):
                    nc.sync.dma_start(
                        out=w_planes[0:P:8].bitcast(I32),
                        in_=w_scales.rearrange("e a q n -> q (e a) n").bitcast(I32),
                    )
            if a == 0:
                nc.sync.dma_start(offs_sb[:], offs)
        nc.sync.dma_start(b_sb[:], b)

        def load_weights(i):
            rows = w_words[W_CUTS[i] : W_CUTS[i + 1]].rearrange("e a p c -> p (e a) c")
            nc.sync.dma_start(out=w_sb[i][:].bitcast(I32), in_=rows.bitcast(I32))

        load_weights(0)
        load_weights(1)
        nc.sync.dma_start(pos_sb[0][:], pos1)
        load_weights(2)
        nc.sync.dma_start(pos_sb[1][:], pos2)
        nc.sync.dma_start(pos_sb[2][:], pos3)

        apart = {}

        def gathered(a, lo, hi):
            for (pass_apart, first), tile in apart.items():
                if pass_apart == a and first <= lo < first + tile.shape[1]:
                    return tile[:, lo - first : hi - first]
            return slot_words[a][:, lo:hi]

        def by_offs(tile, lo, hi):
            window = tile[:, 0 : window_columns(hi - lo)]
            return window.indirect(offs_sb[:, lo // PER_COLUMN : hi // PER_COLUMN])

        def interleave(a, i, vector_tokens, rows):
            lo, hi = X_CUTS[a][i], X_CUTS[a][i + 1]
            mid = lo + vector_tokens
            if mid > lo:
                dst, src = interleaved_views(rounded[a][:, lo:mid, rows], x_sb[a][i][:, rows, 0 : mid - lo])
                nc.vector.tensor_copy(dst, src)
            cuts = [mid, WIDE, hi] if mid < WIDE < hi else [mid, hi]
            for t0, t1 in zip(cuts, cuts[1:]):
                dst, src = interleaved_views(rounded[a][:, t0:t1, rows], x_sb[a][i][:, rows, t0 - lo : t1 - lo])
                nc.scalar.activation(dst, src, COPY)

        def quantize(a, token_cuts):
            for lo, hi in zip(token_cuts, token_cuts[1:]):
                nc.vector.quantize_mx(
                    out=token_words[a][:, lo:hi].bitcast(FP8X4),
                    scales=token_scales[PLANE_STEP * a :, lo:hi],
                    in_=rounded[a][:, lo:hi, :].rearrange("p t j -> p (t j)"),
                )

        def gather_words(a, lo, hi):
            nc.vector.tensor_copy(gathered(a, lo, hi), by_offs(token_words[a], lo, hi))

        def gather_scales(lo, hi, queue, passes):
            nc.vector.tensor_copy(slot_scales[0][:, lo:hi], by_offs(token_scales, lo, hi))
            for a in passes:
                first_row = PLANE_STEP * a
                queue.dma_start(
                    out=slot_scales[a][0:PLANE_ROWS, lo:hi].bitcast(I32),
                    in_=slot_scales[0][first_row : first_row + PLANE_ROWS, lo:hi].bitcast(I32),
                )

        acc = {}

        def multiply(e, a):
            cols = slice(e * C, (e + 1) * C)
            if a == 0:
                bank = e if e < BANKS else e - BANKS
                acc[e] = psum.tile([P, C], F32, name=f"acc{e}", tag=f"bank{bank}")
            load = max(i for i, e0 in enumerate(W_CUTS) if e0 <= e)
            nc.tensor.matmul_mx(
                out=acc[e][:],
                lhsT=w_sb[load][:, (e - W_CUTS[load]) * PASSES + a, :].bitcast(FP4X4),
                lhsT_scale=w_planes[:, e * PASSES + a, :],
                rhs=gathered(a, cols.start, cols.stop).bitcast(FP8X4),
                rhs_scale=slot_scales[a][:, cols],
                start=(a == 0),
                stop=(a == PASSES - 1),
            )
            if a == PASSES - 1:
                nc.scalar.activation(y_sb[:, cols], acc[e][:], SILU, bias=b_sb[:, e : e + 1])
                if e + BANKS < HELD // C:
                    multiply(e + BANKS, 0)

        def last_pass(expert_cuts):
            for e0, e1 in zip(expert_cuts, expert_cuts[1:]):
                gather_words(2, e0 * C, e1 * C)
                for e in range(e0, e1):
                    multiply(e, 2)

        first_row, other_rows, all_rows = slice(0, 1), slice(1, PACK), slice(0, PACK)
        for i in (0, 1):
            interleave(0, i, VECTOR_TOKENS[i], first_row)
        interleave(0, 0, VECTOR_TOKENS[0], other_rows)
        quantize(0, X_CUTS[0][:2])
        interleave(0, 1, VECTOR_TOKENS[1], other_rows)
        interleave(0, 2, VECTOR_TOKENS[2], all_rows)
        quantize(0, X_CUTS[0][1:])
        for a in range(1, PASSES):
            for i in range(len(X_CUTS[a]) - 1):
                interleave(a, i, 0, all_rows)
        for r in range(1, 4):
            nc.scalar.dma_start(out=w_plane_rows[r:P:32], in_=w_plane_rows[8 * r : P : 32])

        gather_words(0, 0, S - C)
        quantize(1, [0, WIDE, T])
        apart[0, S - C] = keep.tile([P, C], U32, name="after_pass1", tag="x1_2", align_bytes=ALIGN)
        gather_words(0, S - C, S)
        gather_words(1, 0, HELD - C)
        quantize(2, [0, WIDE, T])
        apart[1, HELD - C] = keep.tile([P, C], U32, name="after_pass2", tag="x2_1", align_bytes=ALIGN)
        gather_words(1, HELD - C, HELD)
        apart[1, HELD] = keep.tile([P, S - HELD], U32, name="held", tag="rounded2", align_bytes=ALIGN)

        gather_scales(0, FIRST_HALF * C, nc.scalar, (1, 2))
        gather_scales(FIRST_HALF * C, S, nc.sync, (2, 1))

        last_rows = (E - W_CUTS[-2]) * PASSES
        w_sb.append(late.tile([P, last_rows, 2 * N], U8, name="w_last", align_bytes=ALIGN, offset=0))
        load_weights(len(w_sb) - 1)
        gate_sb = late.tile([P, TOP, T], F32, name="gate_sb", align_bytes=ALIGN, offset=last_rows * 2 * N)
        for r in range(TOP):
            nc.sync.dma_start(gate_sb[:, r, :], gate[r])

        for e in range(BANKS):
            multiply(e, 0)
        for e in range(FIRST_HALF):
            multiply(e, 1)
        last_pass([0, W_CUTS[1], FIRST_HALF])
        gather_words(2, FIRST_HALF * C, HELD + C)
        for e in range(FIRST_HALF, HELD // C):
            for a in (1, 2):
                multiply(e, a)
        for e in range(HELD // C, E):
            multiply(e, 0)
        gather_words(1, HELD, S)
        for e in range(HELD // C, E):
            if e > HELD // C:
                gather_words(2, e * C, (e + 1) * C)
            for a in (1, 2):
                multiply(e, a)

        def by_pos(r, tokens):
            return y_sb[:].indirect(pos_sb[r][:, tokens.start // PER_COLUMN : tokens.stop // PER_COLUMN])

        def product(r, tokens):
            nc.vector.tensor_tensor(prod[:, r, tokens], picked[:, r - 1, tokens], gate_sb[:, r, tokens], MULT)

        def first_sum(tokens):
            nc.vector.tensor_tensor(part[:, tokens], prod[:, 0, tokens], prod[:, 1, tokens], ADD)

        def second_sum(tokens):
            nc.vector.tensor_tensor(out_sb[:, tokens], part[:, tokens], prod[:, 2, tokens], ADD)
            nc.sync.dma_start(out[:, tokens], out_sb[:, tokens])

        second = [slice(lo, hi) for lo, hi in zip(SECOND_CUTS, SECOND_CUTS[1:])]
        third = [slice(lo, hi) for lo, hi in zip(THIRD_CUTS, THIRD_CUTS[1:])]
        for r, parts in ((1, second), (2, third)):
            for tokens in parts:
                nc.scalar.activation(picked[:, r - 1, tokens], by_pos(r, tokens), COPY)
        nc.vector.tensor_tensor(prod[:, 0, :], by_pos(0, slice(0, T)), gate_sb[:, 0, :], MULT)
        for tokens in second:
            product(1, tokens)
        first_sum(second[0])
        product(2, third[0])
        first_sum(second[1])
        for done, tokens in zip(third, third[1:]):
            product(2, tokens)
            second_sum(done)
        second_sum(third[-1])
